import numpy as np, ml_dtypes
CORES = [40,41,42,43,44,45,46,47]
N = 8
BF = ml_dtypes.bfloat16
CAP, S, Q, M, W, RO = 64, 512, 16, 3, 4096, 3
def blocks(m):
    return np.stack([m[:, 16 * g:16 * g + 16, 16 * g:16 * g + 16] for g in range(8)], axis=1)
def diag(m):
    z = np.zeros((N, 8, 16, 8, 16), m.dtype)
    for g in range(8): z[:, g, :, g, :] = m[:, g]
    return z.reshape(N, 128, 128)
def play(b, lu, pb, ob):
    live = b[:, :, 0, :] >= 0
    num = np.maximum(np.matmul(pb.swapaxes(2, 3), b), 0)
    h = np.zeros(b.shape, np.int64)
    for j in range(16): h = h + np.take_along_axis(lu, num[:, :, j:j + 1, :], axis=3)
    fire = (np.matmul(ob.swapaxes(2, 3), np.maximum(h, 0)) > 0) & live[:, :, None, :]
    b = np.where(fire, (b + 1) & (Q - 1), b)
    return b, np.where(live, np.add.reduce(b, axis=2) & (N - 1), -1)
def parts(rng):
    cells = np.argsort(rng.random((N, 8, 16, 16)), axis=-1)[..., :M]
    pb = np.zeros((N, 8, 16, 16), np.int64); np.put_along_axis(pb, cells, np.broadcast_to(Q ** np.arange(M), cells.shape), axis=-1)
    lu = np.clip(rng.integers(-127, 128, (N, 8, 16, W)) + rng.integers(-16, 17, (N, 8, 16, 1)), -127, 127)
    return np.ascontiguousarray(pb.swapaxes(2, 3)), lu, rng.integers(-1, 2, (N, 8, 16, 16))
def boards(rng, m):
    return np.where(m[:, :, None, :], rng.integers(0, Q, (N, 8, 16, S)), -1)
def pack(b, lu, pb, ob):
    w = lambda a: np.ascontiguousarray(a).astype(np.float32).astype(BF)
    return {"x": w(b.reshape(N, 128, S)), "lut": w(lu.reshape(N, 128, W)), "pl": w(diag(pb)), "pol": w(diag(ob))}
def setup_inputs(rng):
    pb, lu, ob = parts(rng); fill = rng.choice(np.array([0.6, 0.75, 0.9, 1.0]), (N, 8, 1))
    return pack(boards(rng, rng.random((N, 8, S)) < fill), lu, pb, ob)
def setup_inputs_room(rng):
    pb, lu, ob = parts(rng); lu[:, 7] = -np.abs(lu[:, 7]); pool = rng.integers(0, Q, (N, 8, 16, 3 * S)); to = play(pool, lu, pb, ob)[1]
    b = np.full((N, 8, 16, S), -1, np.int64)
    for a in range(N):
        for g in range(7):
            seq = rng.permutation(N); left = S; ix = [np.zeros(0, np.int64)]
            if a == 0: seq = np.concatenate([np.array([1]), seq[seq != 1]])
            for i in range(N):
                n = int(rng.choice(np.array([0, 1, CAP - 1, CAP, CAP + 1, 2 * CAP])))
                if a == 0 and i == 0: n = (CAP, CAP + 1, 2 * CAP, CAP - 1, 1, 0, CAP)[g]
                if g == 6: n = CAP
                n = min(n, left); left -= n
                if n > 0: ix.append(np.resize(np.flatnonzero(to[a, g] == seq[i]), n).astype(np.int64))
            ix = rng.permutation(np.concatenate(ix)); pos = rng.permutation(S)[:len(ix)]
            b[a, g][:, pos] = pool[a, g][:, ix]
        e = 2 * int(rng.integers(0, N // 2))
        if a == 0: e = 2
        if e == a: e = (a + 2) % N
        some = rng.integers(0, Q, (16, 16 * S)); s = np.add.reduce(some, axis=0) & (N - 1)
        b[a, 7] = some[:, np.concatenate([np.flatnonzero(s == e)[:270], np.flatnonzero(s == e + 1)[:S - 270]])]
    return pack(b, lu, pb, ob)
def setup_inputs_ties(rng):
    pb, lu, ob = parts(rng)
    lu[:, :2] = rng.integers(-1, 2, (N, 2, 16, W)); lu[:, 2] = rng.choice(np.array([-127, 127]), (N, 16, W)); ob[:, 2] = rng.choice(np.array([-1, 1]), (N, 16, 16))
    lu[:, 3] = lu[:, 3, :1]; lu[:, 4] = -np.abs(lu[:, 4]); lu[:, 5] = 127; ob[:, 5] = 1; ob[:, 5, :, 8:] = -1
    ob[:, 6, :, :4] = 0; ob[:, 6, :, 4:8] = -1; ob[:, 6, :, 8:12] = 1
    lu[:, 7] = np.abs(lu[:, 7]); lu[:, 7, 8:] = lu[:, 7, :8]; ob[:, 7, :8, :8] = 1; ob[:, 7, 8:, :8] = -1
    fill = rng.choice(np.array([0.7, 0.9, 1.0]), (N, 8, 1))
    b = boards(rng, rng.random((N, 8, S)) < fill)
    b[:, 4, :, 0] = 0; b[:, 4, :, 1:Q + 1] = Q - 1; b[:, 4, 15, 1:Q + 1] = np.arange(Q)
    b[:, 5, :8, 0] = Q - 1; b[:, 5, 8:, 0] = 0; b[:, 5, :8, 1] = Q - 2; b[:, 5, 8:, 1] = Q - 1
    return pack(b, lu, pb, ob)
def setup_inputs_alike(rng):
    pb, lu, ob = parts(rng); m = rng.random((N, 8, S)) < rng.choice(np.array([0.75, 0.95]), (N, 8, 1)); m[:, :3] = True
    b = boards(rng, m)
    b[:, 0] = b[:, 0, :, :1]; b[:, 1] = np.tile(b[:, 1, :, :2], (1, 1, S // 2)); b[:, 2] = (Q - 1) * rng.integers(0, 2, (N, 1, S))
    pb[:, 4] = pb[:, 4, :, :1]
    return pack(b, lu, pb, ob)
def setup_inputs_thin(rng):
    pb, lu, ob = parts(rng); q = rng.permutation(N); fill = np.zeros((N, 8, 1))
    fill[:, 4:, 0] = np.stack([rng.permutation(np.array([0.1, 0.4, 0.7, 1.0])) for i in range(N)])
    fill[:, 7, 0] = 0.9; fill[q[0]] = 0.0; fill[q[1], 2] = 1.0
    m = rng.random((N, 8, S)) < fill; m[:, 0, S - 1] = True; m[:, 1, 0] = True
    return pack(boards(rng, m), lu, pb, ob)
def setup_inputs_spread(rng):
    pb, lu, ob = parts(rng)
    lu = ((2 * rng.random((N, 8, 16, W)) - 1) * np.exp2(7 * rng.random((N, 8, 1, W)))).astype(np.int64) * (rng.random((N, 8, 1, W)) > 0.0625)
    m = rng.random((N, 8, 1, S)) < rng.choice(np.array([0.3, 0.8, 1.0]), (N, 8, 1, 1))
    v = np.minimum((Q * rng.random((N, 8, 16, S)) ** np.exp2(rng.integers(-2, 3, (N, 8, 16, 1)))).astype(np.int64), Q - 1)
    return pack(np.where(m, v, -1), lu, pb, ob)
def check_inputs(d):
    bad = []; v = {k: np.asarray(d[k]).astype(np.float32) for k in ("x", "lut", "pl", "pol")}
    for k, lo, hi in (("x", -1, Q - 1), ("lut", -127, 127), ("pol", -1, 1)):
        if not np.all((v[k] >= lo) & (v[k] <= hi) & (v[k] == np.floor(v[k]))): bad.append("range of " + k)
    e = v["x"].reshape(N, 8, 16, S) == -1
    if np.any(np.any(e, axis=2) != np.all(e, axis=2)): bad.append("empty slots of x")
    for k in ("pl", "pol"):
        if not np.all(diag(blocks(v[k])) == v[k]): bad.append("zeros outside the blocks of " + k)
    want = np.concatenate([np.zeros(16 - M), Q ** np.arange(M)])
    if not np.all(np.sort(blocks(v["pl"]), axis=2) == want[:, None]): bad.append("weights of pl")
    return bad
def reference(x, lut, pl, pol):
    whole = lambda a: a.astype(np.float32).astype(np.int64)
    b = whole(x).reshape(N, 8, 16, S); lu = whole(lut).reshape(N, 8, 16, W); pb = blocks(whole(pl)); ob = blocks(whole(pol))
    for ply in range(RO):
        b, to = play(b, lu, pb, ob)
        come = np.full((N, 8, 16, S), -1, np.int64)
        for a in range(N):
            for r in range(N):
                for g in range(8):
                    ix = np.flatnonzero(to[a, g] == r)[:CAP]
                    come[r, g, :, a * CAP:a * CAP + len(ix)] = b[a, g][:, ix]
        b = come
    return {"y": b.reshape(N, 128, S).astype(np.float32).astype(BF)}

@@ -1,0 +1,491 @@
+from concourse.bass import DstId, RemoteDMATransfer
+from concourse.mybir import AluOpType as ALU, ActivationFunctionType as ACT
+
+N, S, CAP, RO, LW = 8, 512, 64, 3, 4096
+NS = 2
+GS = 8 // NS
+W = 16 * GS
+Z = 128 - W
+C = S // NS
+NCC = C // 128
+NB = C // 64
+TW = NCC * 64
+BW = TW // 4
+KC = C // 16
+SW = 5120
+TB = LW + 16
+UC = 16
+MAGIC = 12582912.0
+OFFS = 64
+CHUNKS = [[0, 1], [2], [3]]
+NUMS = [[[0]], [[1]], [[2, 3]]]
+CALLS = [[(2, 8), (1, 4), (3, 4)], [(4, 4), (6, 4), (5, 4), (7, 4)]]
+CALLS_LAST = CALLS
+PAR = {"gb": 1.13, "g0": 0.0, "theta": 0.21, "bias": 1.59, "c": 1.56, "sc": 3.8, "f": 1.2, "pe": 0.00042, "lat": 0.1,
+       "fix": 0.05, "row": 0.03, "bw": 20000.0, "dma0": 1.5, "call": 0.4, "first": 1.0, "wake": 0.2,
+       "pri": {"idn": 40, "zf": 20, "ones": 50, "polz": 45, "pidx": 30, "elc": 30, "lqc": 30, "pq": 30, "pqf": 30,
+               "els": 30, "lq": 30, "wr": -1.6, "polh": -1.9, "pt": 5.4, "off": -2.2, "sz": 4.1, "snd": 1.5,
+               "pnum": 0.3, "pw": 3.4, "ph": 0.5, "uu": 0.4}}
+
+
+def blk_rel(rel):
+    return (rel & 1) + 2 * (rel // (2 * NS)) if NCC > 1 else rel & 1
+
+
+BF, F32, F16 = "bfloat16", "float32", "float16"
+SCRATCH = {k: ("sbuf", [128, n], d) for k, n, d in [
+    ("xs", NS * S, BF), ("tab", NS * TB, BF), ("gat", NS * C * 16, BF), ("snd", NS * RO * SW, BF), ("lnd", NS * RO * S, BF),
+    ("zpl", Z + NS * 128, BF), ("polb", NS * 128, BF), ("polh", NS * 128, F16), ("ones", 256, BF), ("eig", 256, BF),
+    ("kth", 128, BF), ("idn", 128, BF), ("zf", 2 * Z + W, BF), ("zsel", (2 * NCC - 1) * 64, BF), ("negr", TW, BF),
+    ("tri", 128, BF), ("creg", TW, BF), ("dmp", TW, F32), ("kmk", TW, BF), ("pidx", 8, "int32"), ("pq", 8, "int32"),
+    ("pqf", 8, F32), ("elc", 16, F32), ("els", 16, "uint16"), ("lqc", 240, F32), ("lq", 240, F16), ("cw", 256, BF),
+    ("off", NS * C, "uint16"), ("rel", NS * C, F16), ("vv", NS * C, BF), ("wr", NS * C, BF), ("uu", NS * TW, BF),
+    ("mb", NS * (3 * BW + TW), BF), ("scn", NS * TW, F32), ("ee", NS * TW, F16), ("pos", NS * KC, "uint16"),
+    ("yo", NS * C, BF)]}
+for _b in ("pnum", "ph0", "ph1", "pw0", "pw1", "pt0", "pt1", "pa"):
+    SCRATCH[_b] = ("psum", [128, 512], F32)
+
+SEMAPHORES = ["eV", "eS", "eP", "eG", "sent"]
+SEMAPHORES += ["ar%d_%d_%d" % (s, t, b) for s in range(NS) for t in range(RO) for b in range(NB if t < RO - 1 else 1)]
+SEMAPHORES += ["d%d" % i for i in range(NS * (1 + 4 * NS))]
+
+
+def build(T, rank, core, topo, P):
+    ops = []
+    cyc = 0.00083 * P["f"]
+    ndma = [0]
+
+    def add(eng, fn, R, Wr, dur, **kw):
+        o = {"eng": eng, "fn": fn, "R": R, "W": Wr, "dur": dur, "i": len(ops), "s": 0, "fill": False}
+        o.update(kw)
+        ops.append(o)
+
+    def vec(fn, R, Wr, n, **kw):
+        add("V", fn, R, Wr, P["fix"] + max(64, n) * cyc, **kw)
+
+    def gp(fn, R, Wr, n, base=0.15, **kw):
+        add("G", fn, R, Wr, base + 2 * n * cyc, **kw)
+
+    def pe(mms, R, Wr, **kw):
+        def fn(q):
+            ins = None
+            for m in mms: ins = q.matmul(m[0], m[1], m[2], m[3], m[4])
+            return ins
+        add("P", fn, R, Wr, 0.02 + sum(max(64, m[5]) for m in mms) * P["pe"] * P["f"], **kw)
+
+    def dma(eng, out, in_, R, Wr, rows, nbytes, **kw):
+        ndma[0] += 1
+        add(eng, lambda q: q.dma_start(out, in_), R, Wr, 0.06, sem="d%d" % (ndma[0] - 1), rows=rows, nb=nbytes, **kw)
+
+    vec(lambda q: q.memset(T.polb[:], 0.0), [], ["polz"], NS * 64)
+    for s in range(NS):
+        r0, r1 = s * W, (s + 1) * W
+        b0 = Z + s * 128
+        first = s == 0
+        dma("S" if first else "Y", T.xs[0:W, s * S:(s + 1) * S], T.x[r0:r1, :], [], ["xs%d" % s], W, 2 * S, order=10 * s)
+        dma("Y", T.zpl[0:W, b0:b0 + W], T.pl[r0:r1, r0:r1], [], ["zpl%d.0" % s], W, 2 * W, order=10 * s)
+        for i in range(NS):
+            dma("S" if first and i % 2 else "Y", T.tab[i * W:(i + 1) * W, s * TB + 16:(s + 1) * TB], T.lut[r0:r1, :], [],
+                ["tab%d.%d" % (s, i)], W, 2 * LW, order=10 * s + 1)
+        for i in range(NS):
+            dma("Y", T.polb[i * W:(i + 1) * W, s * 128 + i * W:s * 128 + (i + 1) * W], T.pol[r0:r1, r0:r1], ["polz"],
+                ["polb%d.%d" % (s, i)], W, 2 * W, order=10 * s + 2)
+    for s in range(NS):
+        for i in range(1, NS):
+            dma("Y", T.zpl[i * W:(i + 1) * W, Z + s * 128:Z + s * 128 + W], T.pl[s * W:(s + 1) * W, s * W:(s + 1) * W], [],
+                ["zpl%d.%d" % (s, i)], W, 2 * W, order=100 + s)
+
+    for k in range(NS + 1):
+        vec(lambda q, k=k: q.memset(T.zpl[:, k * 128:k * 128 + Z], 0.0), [], ["zplz%d" % k], Z // 2)
+    vec(lambda q: q.memset(T.ones[:], 1.0), [], ["ones"], 128)
+    vec(lambda q: q.memset(T.eig[:], 0.125), [], ["eig"], 128)
+    vec(lambda q: q.memset(T.kth[:], 1.0 / 1024), [], ["kth"], 64)
+    vec(lambda q: q.memset(T.cw[0:64, :], 0.0), [], ["cw"], 64)
+    vec(lambda q: q.memset(T.cw[0:1, 128:256], 0.5), [], ["cw"], 64)
+    vec(lambda q: q.memset(T.cw[0:1, 0:128], OFFS + 0.5), [], ["cw"], 64)
+    vec(lambda q: q.memset(T.cw[32:33, :], -2.0 ** -17), [], ["cw"], 64)
+    gp(lambda q: q.affine_select(T.idn[:], T.ones[:, 0:128], [[-1, 128]], ALU.is_equal, 0.0, 0, 1), ["ones"], ["idn"], 128)
+    vec(lambda q: q.memset(T.zf[:], 0.0), [], ["zf%d" % i for i in range(NS)], Z + W // 2)
+    for i in range(NS):
+        vec(lambda q, i=i: q.tensor_copy(T.zf[i * W:(i + 1) * W, Z:Z + W], T.idn[i * W:(i + 1) * W, i * W:(i + 1) * W]), ["idn"], ["zf%d" % i], 32)
+    sw, so = (2 * NCC - 1) * 8, 128 * (NCC - 1)
+    gp(lambda q: q.affine_select(T.zsel[:], T.eig[:, 0:sw * 8], [[-16, sw], [0, 8]], ALU.is_ge, 0.0, so, 1), ["eig"], ["zsel"], sw * 8)
+    gp(lambda q: q.affine_select(T.zsel[:], T.zsel[:], [[16, sw], [0, 8]], ALU.is_ge, 0.0, 15 - so, -1), ["zsel"], ["zsel"], sw * 8)
+    flag = {"allow_small_or_imprecise_dtypes": True}
+    gp(lambda q: q.iota(T.negr[:], [[0, TW // 8], [-1, 8]], 0, 0, **flag), [], ["negr"], TW)
+    gp(lambda q: q.affine_select(T.tri[:], T.ones[:, 0:128], [[1, 128]], ALU.is_gt, 0.0, 0, -1), ["ones"], ["tri"], 128)
+    gp(lambda q: q.affine_select(T.tri[:], T.tri[:], [[1, 128]], ALU.not_equal, -8192.0, 0, -1), ["tri"], ["tri"], 128)
+    gp(lambda q: q.iota(T.creg[:], [[0, TW // 8], [4, 8]], 48, 0, **flag), [], ["creg"], TW)
+    gp(lambda q: q.iota(T.dmp[:], [[256, 4], [0, BW]], 2048, 2, **flag), [], ["dmp"], TW)
+    gp(lambda q: q.affine_select(T.dmp[:], T.dmp[:], [[0, TW // 8], [1, 8]], ALU.is_equal, -10000.0, 0, 0), ["dmp"], ["dmp"], TW)
+    gp(lambda q: q.affine_select(T.kmk[:], T.ones[:, 0:TW], [[0, TW // 8], [-16, 8]], ALU.is_ge, 0.0, 0, 1), ["ones"], ["kmk"], TW)
+    gp(lambda q: q.affine_select(T.kmk[:], T.kmk[:], [[0, TW // 8], [16, 8]], ALU.is_ge, 0.0, 15, -1), ["kmk"], ["kmk"], TW)
+    gp(lambda q: q.iota(T.pidx[:, 0:2], [[0, 2]], 0, 1), [], ["pidx"], 2)
+    ec = TW // 16
+    gp(lambda q: q.iota(T.elc[:, 0:ec], [[8 if NCC == 2 else 16, ec]], 7, 0, **flag), [], ["elc"], ec)
+    gp(lambda q: q.iota(T.lqc[:], [[1, 240]], -112, 0, **flag), [], ["lqc"], 240)
+    vec(lambda q: q.tensor_scalar(T.pq[:, 0:1], T.pidx[:, 0:1], 8, None, ALU.bitwise_and), ["pidx"], ["pq0"], 1)
+    vec(lambda q: q.tensor_scalar(T.pq[:, 1:2], T.pidx[:, 1:2], 15, None, ALU.bitwise_and), ["pidx"], ["pq1"], 1)
+    vec(lambda q: q.tensor_scalar(T.pqf[:, 0:1], T.pq[:, 0:1], 8.0 if NCC == 2 else 1.0, None, ALU.mult), ["pq0"], ["pqf0"], 1)
+    vec(lambda q: q.tensor_copy(T.pqf[:, 1:2], T.pq[:, 1:2]), ["pq1"], ["pqf1"], 1)
+    vec(lambda q: q.tensor_scalar(T.els[:, 0:ec], T.elc[:, 0:ec], T.pqf[:, 0:1], None, ALU.add), ["elc", "pqf0"], ["els"], ec)
+    vec(lambda q: q.tensor_scalar(T.lq[:], T.lqc[:], T.pqf[:, 1:2], None, ALU.is_equal), ["lqc", "pqf1"], ["lq"], 240)
+    mbw = 3 * BW + TW
+    for s in range(NS):
+        vec(lambda q, s=s: q.memset(T.mb[:, s * mbw:s * mbw + 3 * BW], 0.0), [], ["mbz%d" % s], 48, s=s)
+        vec(lambda q, s=s: q.memset(T.tab[:, s * TB:s * TB + 16], 0.0), [], ["tabz%d" % s], 8, s=s)
+        vec(lambda q, s=s: q.tensor_scalar(T.polh[:, s * 128:(s + 1) * 128], T.polb[:, s * 128:(s + 1) * 128], 2.0 ** -8, None, ALU.mult),
+            ["polz"] + ["polb%d.%d" % (s, i) for i in range(NS)], ["polh%d" % s], 64, s=s)
+    for t in range(RO):
+        for s in range(NS):
+            for r in range(N):
+                a = (s * RO + t) * SW + r * 512
+                gp(lambda q, a=a: q.iota(T.snd[:, a:a + CAP], [[0, CAP]], 0, 0, **flag), [], ["sz%d.%d.%d" % (s, t, r)], CAP,
+                   base=0.13, s=s, fill=True)
+
+    zplz = ["zplz%d" % k for k in range(NS + 1)]
+    kb_own = blk_rel(rank)
+    cnt = [0]
+
+    def came(s, t, a):
+        if a == rank:
+            o = (s * RO + t) * SW + rank * 512
+            return T.snd[:, o:o + CAP]
+        o = (s * RO + t) * S + a * CAP
+        return T.lnd[:, o:o + CAP]
+
+    def ply(s, t):
+        c0 = s * C
+
+        def merged(out, kb, mat, m0, first, last):
+            mms = []
+            for i in range(NS):
+                a = 2 * ((kb // 2) * NS + i) + kb % 2
+                lo = m0 - i * W
+                if t == 0: mms.append([out, mat[0:W, lo:lo + 128], T.xs[0:W, s * S + a * CAP:s * S + (a + 1) * CAP], False, False, 64])
+                else: mms.append([out, mat[:, lo:lo + 128], came(s, t - 1, a), False, False, 64])
+            mms[0][3] = first
+            mms[-1][4] = last
+            return mms
+
+        def src(b):
+            if t == 0: return ["xs%d" % s], None
+            return ["snd%d.%d" % (s, t - 1)], (s, t - 1, b)
+
+        def span(ch):
+            return min(kb_own ^ b for b in ch) * 64, max(kb_own ^ b for b in ch) * 64 + 64
+
+        for grp in (NUMS if t else [[list(range(NB))]]):
+            for ch in grp:
+                for b in ch:
+                    kb = kb_own ^ b
+                    R, ext = src(b)
+                    zp = ["zpl%d.%d" % (s, i) for i in (range(NS) if t else [0])]
+                    pe(merged(T.pnum[:, kb * 64:kb * 64 + 64], kb, T.zpl, Z + s * 128, True, True), R + zp + zplz, ["pnum"], s=s, ext=ext)
+            for ch in grp:
+                lo, hi = span(ch)
+                vec(lambda q, lo=lo, hi=hi: q.tensor_scalar(T.off[:, c0 + lo:c0 + hi], T.pnum[:, lo:hi],
+                                                            16 - 273.0 * OFFS if t else 16.0, 0.0, ALU.add, ALU.max),
+                    [], ["pnum"] + ["off%d.%d" % (s, b) for b in ch], hi - lo, s=s)
+        ptn = "pt%d" % (s % 2)
+        pt = T[ptn]
+        pe([[pt[:, 0:TW], T.kth[:], T.negr[:], True, False, TW]], ["kth", "negr"], [ptn], s=s)
+        pe([[T.pa[:, 0:TW], T.ones[:, 0:128], T.creg[:], True, False, TW]], ["ones", "creg"], ["pa"], s=s)
+        done = []
+        for ch in CHUNKS:
+            hn, wn = "ph%d" % (cnt[0] % 2), "pw%d" % (cnt[0] % 2)
+            cnt[0] += 1
+            ph, pw = T[hn], T[wn]
+            lo, hi = span(ch)
+            for b in ch:
+                kb = kb_own ^ b
+                for u in range(64 // UC):
+                    add(("V", "S"), None, ["off%d.%d" % (s, b), "tabz%d" % s] + ["tab%d.%d" % (s, i) for i in range(NS)],
+                        ["gat%d.%d.%d" % (s, b, u)], UC * 16 * P["c"] * cyc, s=s, fill=True, gat=(s, t, b, u), col=c0 + kb * 64 + u * UC)
+                g0 = (c0 + kb * 64) * 16
+                for hf in range(2):
+                    pe([[ph[:, kb * 64:kb * 64 + 64], T.idn[:], T.gat[:, g0 + j:g0 + 1024:16], j == 0, j == 15, 64]
+                        for j in range(hf * 8, hf * 8 + 8)], ["idn"] + ["gat%d.%d.%d" % (s, b, u) for u in range(64 // UC)], [hn], s=s)
+            nm = "%d.%d" % (s, ch[0])
+            vec(lambda q, ph=ph, lo=lo, hi=hi: q.tensor_scalar(T.rel[:, c0 + lo:c0 + hi], ph[:, lo:hi], 0.0, 2.0 ** -8, ALU.max, ALU.mult),
+                [], [hn, "rel" + nm], hi - lo, s=s)
+            for b in ch:
+                kb = kb_own ^ b
+                R, ext = src(b)
+                o = pw[:, kb * 64:kb * 64 + 64]
+                pe([[o, T.cw[0:64, min(t, 1) * 128:min(t, 1) * 128 + 128], T.ones[0:64, 0:64], True, False, 64]]
+                   + merged(o, kb, T.zf, Z, False, False), R + ["cw", "ones"] + ["zf%d" % i for i in range(NS)], [wn], s=s, ext=ext)
+                pe([[o, T.polh[:, s * 128:(s + 1) * 128], T.rel[:, c0 + kb * 64:c0 + kb * 64 + 64], False, True, 64]],
+                   ["polh%d" % s, "rel" + nm], [wn], s=s)
+            vec(lambda q, pw=pw, lo=lo, hi=hi: q.tensor_scalar(T.vv[:, c0 + lo:c0 + hi], pw[:, lo:hi], MAGIC, MAGIC, ALU.add, ALU.subtract),
+                [], [wn, "vv" + nm], hi - lo, s=s)
+            before = len(done) // 2
+            done += ch
+            for cr in range(before, len(done) // 2):
+                cc = (kb_own // 2) ^ cr
+                z0 = (NCC - 1 - cc) * 64
+                pe([[pt[:, 0:TW], T.vv[:, c0 + cc * 128:c0 + cc * 128 + 128], T.zsel[:, z0:z0 + TW], False, cr == NCC - 1, TW]],
+                   ["zsel"] + ["vv%d.%d" % (s, x[0]) for x in CHUNKS if x[0] in done], [ptn], s=s)
+        vvs = ["vv%d.%d" % (s, x[0]) for x in CHUNKS]
+        t0, m0 = s * TW, s * mbw
+        vec(lambda q: q.tensor_scalar(T.wr[:, c0:c0 + C], T.vv[:, c0:c0 + C], OFFS + 16.0, -16.0, ALU.is_ge, ALU.mult), vvs, ["wr%d" % s], C // 2, s=s)
+        vec(lambda q: q.tensor_scalar(T.uu[:, t0:t0 + TW], pt[:, 0:TW], 128.0, None, ALU.max), [], [ptn, "uu%d" % s], TW, s=s)
+        vec(lambda q: q.tensor_tensor(T.mb[:, m0 + 3 * BW:m0 + mbw], pt[:, 0:TW], T.uu[:, t0:t0 + TW], ALU.is_equal),
+            ["uu%d" % s], [ptn, "mb%d" % s], TW, s=s)
+        pe([[T.pa[:, 0:TW], T.ones[:, 0:128] if j else T.tri[:], T.mb[:, m0 + (3 - j) * BW:m0 + (3 - j) * BW + TW], False, j == 3, TW]
+            for j in range(4)], ["mb%d" % s, "mbz%d" % s, "tri", "ones"], ["pa"], s=s)
+        vec(lambda q: q.tensor_tensor_scan(T.scn[:, t0:t0 + TW], T.dmp[:], T.pa[:, 0:TW], -10000.0, ALU.max, ALU.min),
+            ["dmp"], ["pa", "scn%d" % s], TW, s=s)
+        vec(lambda q: q.tensor_tensor(T.ee[:, t0:t0 + TW], T.scn[:, t0:t0 + TW].indirect(T.els[:, 0:ec]), T.kmk[:], ALU.mult),
+            ["scn%d" % s, "els", "kmk"], ["ee%d" % s], TW * max(2, P["c"]), s=s)
+        pe([[pt[:, 0:KC], T.lq[:, 112 - 16 * h:240 - 16 * h], T.ee[:, t0 + h * KC:t0 + (h + 1) * KC], h == 0, h == 7, KC] for h in range(8)],
+           ["lq", "ee%d" % s], [ptn], s=s)
+        vec(lambda q: q.tensor_scalar(T.pos[:, s * KC:(s + 1) * KC], pt[:, 0:KC], 2048.0, None, ALU.add), [], [ptn, "pos%d" % s], KC, s=s)
+        w0 = (s * RO + t) * SW
+        vec(lambda q: q.tensor_tensor(T.snd[:, w0:w0 + SW].indirect(T.pos[:, s * KC:(s + 1) * KC]), T.vv[:, c0:c0 + C], T.wr[:, c0:c0 + C], ALU.add),
+            vvs + ["wr%d" % s, "pos%d" % s] + ["sz%d.%d.%d" % (s, t, r) for r in range(N)], ["snd%d.%d" % (s, t)], C * P["sc"], s=s)
+        last = t == RO - 1
+        for call in (CALLS_LAST if last else CALLS):
+            def send(q, call=call):
+                trs, e0 = [], 0
+                for rel, ne in call:
+                    dst = T.cores[rank ^ rel]
+                    rid, pid = topo.addr(dst)[0:2]
+                    eng = topo.engines(core, dst)[e0:e0 + ne]
+                    e0 += ne
+                    o = w0 + (rank ^ rel) * 512
+                    lo = (s * RO + t) * S + rank * CAP
+                    trs.append(RemoteDMATransfer(dst_ids=[DstId(rid=rid, pnc=pid)], dma_engine_mask=sum(1 << e for e in eng),
+                                                 remote_sem=T.sem["ar%d_%d_%d" % (s, t, 0 if last else blk_rel(rel))],
+                                                 src=T.snd[:, o:o + CAP], dst=T.lnd[:, lo:lo + CAP]))
+                return q.remote_dma_fused(trs, local_sem=T.sem.sent)
+            add("G", send, ["snd%d.%d" % (s, t)], [], P["call"], s=s, call=call, st=(s, t))
+
+    for t in range(RO):
+        for s in range(NS):
+            ply(s, t)
+
+    for s in range(NS):
+        mms = []
+        for kb in range(NB):
+            for i in range(NS):
+                mms.append([T.pnum[:, kb * 64:kb * 64 + 64], T.zf[:, Z - i * W:Z - i * W + 128], came(s, RO - 1, i * NB + kb), i == 0, i == NS - 1, 64])
+        pe(mms, ["snd%d.%d" % (s, RO - 1)], ["pnum"], s=s, ext=(s, RO - 1, 0))
+        vec(lambda q, s=s: q.tensor_scalar(T.yo[:, s * C:(s + 1) * C], T.pnum[:, 0:C], -float(OFFS), -1.0, ALU.add, ALU.max),
+            [], ["pnum", "yo%d" % s], C, s=s)
+        for i in range(NS):
+            dma("S" if s == NS - 1 and i % 2 else "Y", T.y[s * W:(s + 1) * W, i * C:(i + 1) * C], T.yo[i * W:(i + 1) * W, s * C:(s + 1) * C],
+                ["yo%d" % s], [], W, 2 * C, order=1000 + s, s=s, store=True)
+    return ops
+
+
+def arrive_count(t, b):
+    last = t == RO - 1
+    return sum(ne for call in (CALLS_LAST if last else CALLS) for rel, ne in call if last or blk_rel(rel) == b)
+
+
+def depend(ops):
+    lastw, readers, sends = {}, {}, {}
+    for o in ops:
+        d = set()
+        for r in o["R"]:
+            if r in lastw: d.add(lastw[r])
+        for w in o["W"]:
+            if w in lastw: d.add(lastw[w])
+            d.update(readers.get(w, []))
+        for r in o["R"]: readers.setdefault(r, []).append(o["i"])
+        for w in o["W"]:
+            lastw[w] = o["i"]
+            readers[w] = []
+        d.discard(o["i"])
+        o["deps"] = sorted(d)
+        if "call" in o: sends.setdefault(o["st"], []).append(o["i"])
+        o["xd"] = sends[o["ext"][0:2]] if o.get("ext") else []
+    dm = sorted((o["order"], o["i"]) for o in ops if "sem" in o)
+    for q in ("Y", "S"):
+        seq = [i for _, i in dm if ops[i]["eng"] == q]
+        for a, b in zip(seq, seq[1:]): ops[b]["after"] = a
+
+
+def timing(ops, P):
+    fin, eng_of, arr = {}, {}, {}
+    free = {e: 0.0 for e in "VSPGY"}
+    st = {"first": True, "eng": [0.0] * 16, "prev": {}}
+
+    def ready(o, e):
+        t = 0.0
+        for d in o["deps"]:
+            t = max(t, fin[d] + (0.0 if eng_of[d] == e == "P" else P["wake"] if "sem" in ops[d] else P["lat"]))
+        if o["xd"]: t = max(t, arr[o["ext"]] + P["wake"])
+        return t
+
+    def length(o, e):
+        if "gat" not in o: return o["dur"]
+        p = st["prev"].get(e)
+        joined = p is not None and "gat" in p and p["gat"][0:3] == o["gat"][0:3] and abs(p["gat"][3] - o["gat"][3]) == 1
+        return o["dur"] + (0.0 if joined else 0.06)
+
+    def commit(o, e, t):
+        d = length(o, e)
+        free[e] = t + d
+        fin[o["i"]] = t + d
+        eng_of[o["i"]] = e
+        st["prev"][e] = o
+        if "sem" in o:
+            b = max([t + P["dma0"]] + st["eng"]) + max(1, o["rows"] / 16) * (P["row"] + o["nb"] / P["bw"])
+            st["eng"] = [b] * 16
+            fin[o["i"]] = b
+        if "call" in o:
+            t0 = t + d + P["dma0"] + (P["first"] if st["first"] else 0.0)
+            st["first"] = False
+            e0 = 0
+            for rel, ne in o["call"]:
+                b = max([t0] + st["eng"][e0:e0 + ne]) + 128 / ne * (P["row"] + 128 / P["bw"])
+                for k in range(e0, e0 + ne): st["eng"][k] = b
+                e0 += ne
+                key = o["st"] + (0 if o["st"][1] == RO - 1 else blk_rel(rel),)
+                arr[key] = max(arr.get(key, 0.0), b)
+    return ready, length, commit, free, fin
+
+
+def schedule(ops, P):
+    n = len(ops)
+    succ = [[] for _ in ops]
+    for o in ops:
+        for d in o["deps"]: succ[d].append((o["i"], P["lat"] + (P["dma0"] + o["dur"] if "sem" in ops[d] else 0.0)))
+        for d in o["xd"]: succ[d].append((o["i"], P["dma0"] + 1.0 + 0.4 * o["ext"][2]))
+    lev = [0.0] * n
+    for i in range(n - 1, -1, -1):
+        lev[i] = ops[i]["dur"] + max([lev[j] + x for j, x in succ[i]] + [0.0])
+    for o in ops:
+        lev[o["i"]] -= P["bias"] * o["s"] * 2 / NS
+        if "gat" in o: lev[o["i"]] -= P["gb"] * o["gat"][2] + P["g0"]
+        elif o["W"]: lev[o["i"]] += P["pri"].get(o["W"][-1].rstrip("0123456789."), 0.0)
+    ready, length, commit, free, fin = timing(ops, P)
+    need = lambda o: o["deps"] + o["xd"] + ([o["after"]] if "after" in o else [])
+    left = set(range(n))
+    order = []
+    while left:
+        rdy = [ops[i] for i in sorted(left) if all(d not in left for d in need(ops[i]))]
+        isr = set(o["i"] for o in rdy)
+        memo = {}
+
+        def soon(o, e, depth):
+            if o["i"] in isr: return max(ready(o, e), free[e])
+            if depth == 0 or o["xd"] and any(d in left for d in o["xd"]): return None
+            key = o["i"]
+            if key in memo: return memo[key]
+            t = 0.0
+            for d in need(o):
+                if d not in left:
+                    t = max(t, fin[d] + P["lat"])
+                    continue
+                p = ops[d]
+                x = None if p["fill"] or p["eng"] != "P" else soon(p, "P", depth - 1)
+                if x is None:
+                    t = None
+                    break
+                t = max(t, x + p["dur"] + (P["lat"] if e != "P" else 0.0))
+            memo[key] = t
+            return t
+
+        best, forced = None, None
+        for e in "PVSGY":
+            cand = [(max(ready(o, e), free[e]), o) for o in rdy if e in o["eng"]]
+            if not cand: continue
+            t0 = min(c[0] for c in cand)
+            now = [c for c in cand if c[0] <= t0 + 0.001]
+            sgn = 1 if e == "V" else -1
+            t, o = max(now, key=lambda c: (round(lev[c[1]["i"]], 3), sgn * c[1]["i"]))
+            end = t + length(o, e)
+            better = [c for c in cand if lev[c[1]["i"]] > lev[o["i"]] + 0.001 and not c[1]["fill"] and c[0] + P["theta"] < end]
+            if better: t, o = min(better, key=lambda c: c[0])
+            wait = False
+            if e == "V" and o["fill"]:
+                for i in left:
+                    p = ops[i]
+                    if p["eng"] == "V" and i not in isr and not p["fill"] and lev[i] > lev[o["i"]]:
+                        x = soon(p, "V", 3)
+                        if x is not None and x + P["theta"] < end:
+                            wait = True
+                            break
+            if forced is None or t < forced[0]: forced = (t, o, e)
+            if not wait and (best is None or t < best[0]): best = (t, o, e)
+        t, o, e = best or forced
+        commit(o, e, t)
+        left.discard(o["i"])
+        order.append((o["i"], e))
+    return order, max(fin.values())
+
+
+PLAN = {}
+
+
+def rank_program(g, core, T, topo):
+    rank = T.rank_of(core)
+    if rank is None:
+        return
+    ops = build(T, rank, core, topo, PAR)
+    depend(ops)
+    if "order" not in PLAN: PLAN["order"] = schedule(ops, PAR)[0]
+    queues = {"V": g.vector, "S": g.scalar, "P": g.tensor, "G": g, "Y": g.sync}
+    items, item_of, lastq = [], {}, {}
+    for i, e in PLAN["order"]:
+        o, p = ops[i], lastq.get(e)
+        if "gat" in o and p is not None and "gat" in p["ops"][-1] and p["ops"][-1]["gat"][0:3] == o["gat"][0:3] \
+                and abs(p["ops"][-1]["gat"][3] - o["gat"][3]) == 1 and all(d in p["deps"] or d in p["seen"] for d in o["deps"]):
+            p["ops"].append(o)
+        else:
+            p = {"ops": [o], "e": e, "k": len(items), "deps": set(o["deps"]), "seen": set(item_of), "inc": False}
+            items.append(p)
+            lastq[e] = p
+        p["deps"].update(o["deps"])
+        item_of[i] = p
+    known = {e: {} for e in queues}
+    for p in items:
+        e, kn, waits = p["e"], known[p["e"]], []
+        for d in sorted(set(item_of[d]["k"] for d in p["deps"]), reverse=True):
+            dp = items[d]
+            key = dp["ops"][0].get("sem", dp["e"])
+            if key == e == "P" or kn.get(key, -1) >= d: continue
+            dp["inc"] = True
+            waits.append(dp)
+            for k2, v in dp["clock"].items(): kn[k2] = max(kn.get(k2, -1), v)
+            kn[key] = max(kn.get(key, -1), d)
+        ext = p["ops"][0].get("ext")
+        if ext and ext not in kn:
+            kn[ext] = 0
+            waits.append({"ext": ext})
+        p["waits"] = waits
+        p["clock"] = dict(kn)
+    count = {e: 0 for e in queues}
+    sent = 0
+    for p in items:
+        e, q, o = p["e"], queues[p["e"]], p["ops"][0]
+        for w in p["waits"]:
+            if "ext" in w:
+                q.wait_ge(T.sem["ar%d_%d_%d" % w["ext"]], arrive_count(w["ext"][1], w["ext"][2]))
+            elif "sem" in w["ops"][0]:
+                q.wait_ge(T.sem[w["ops"][0]["sem"]], 16)
+            else:
+                q.wait_ge(T.sem["e" + w["e"]], w["n"])
+        if "gat" in o:
+            s = o["gat"][0]
+            lo = min(x["col"] for x in p["ops"])
+            hi = lo + UC * len(p["ops"])
+            win = T.tab[:, s * TB:(s + 1) * TB].indirect(T.off[:, lo:hi])
+            out = T.gat[:, lo * 16:hi * 16]
+            ins = q.tensor_copy(out, win) if e == "V" else q.activation(out, win, ACT.Copy)
+        else:
+            ins = o["fn"](q)
+        if "sem" in o:
+            ins.then_inc(T.sem[o["sem"]], 16)
+        elif "call" in o:
+            sent += sum(ne for rel, ne in o["call"])
+        elif p["inc"]:
+            count[e] += 1
+            p["n"] = count[e]
+            ins.then_inc(T.sem["e" + e], 1)
+    g.wait_ge(T.sem.sent, sent)
+    for o in ops:
+        if o.get("store"): queues[o["eng"]].wait_ge(T.sem[o["sem"]], 16)

@@ -3,51 +3,35 @@ from concourse.mybir import AluOpType as ALU, ActivationFunctionType as ACT
 
 N, S, CAP, RO, LW = 8, 512, 64, 3, 4096
 NS = 2
-GS = 8 // NS
-W = 16 * GS
-Z = 128 - W
-C = S // NS
-NCC = C // 128
-NB = C // 64
-TW = NCC * 64
-BW = TW // 4
-KC = C // 16
+W = 64
+C = 256
 SW = 5120
 TB = LW + 16
-UC = 16
+GAP = 72
+OFFS = 132
+HALF = 0.5 - 2.0 ** -16
 MAGIC = 12582912.0
-OFFS = 64
-CHUNKS = [[0, 1], [2], [3]]
-NUMS = [[[0]], [[1]], [[2, 3]]]
-CALLS = [[(2, 8), (1, 4), (3, 4)], [(4, 4), (6, 4), (5, 4), (7, 4)]]
-CALLS_LAST = CALLS
-PAR = {"gb": 1.13, "g0": 0.0, "theta": 0.21, "bias": 1.59, "c": 1.56, "sc": 3.8, "f": 1.2, "pe": 0.00042, "lat": 0.1,
-       "fix": 0.05, "row": 0.03, "bw": 20000.0, "dma0": 1.5, "call": 0.4, "first": 1.0, "wake": 0.2,
-       "pri": {"idn": 40, "zf": 20, "ones": 50, "polz": 45, "pidx": 30, "elc": 30, "lqc": 30, "pq": 30, "pqf": 30,
-               "els": 30, "lq": 30, "wr": -1.6, "polh": -1.9, "pt": 5.4, "off": -2.2, "sz": 4.1, "snd": 1.5,
-               "pnum": 0.3, "pw": 3.4, "ph": 0.5, "uu": 0.4}}
-
-
-def blk_rel(rel):
-    return (rel & 1) + 2 * (rel // (2 * NS)) if NCC > 1 else rel & 1
-
+UC = 4
+CALLS = [[(1, 16)], [(2, 8), (3, 8)], [(4, 8), (5, 8)], [(6, 8), (7, 8)]]
+PAR = {"c": 1.56, "sc": 3.8, "f": 1.0, "pe": 0.00042, "lat": 0.2, "room": 0.0, "join": 0.1, "lean": 0.0, "mm": 2, "split": [3],
+       "row": 0.03, "bw": 20000.0, "dma0": 1.0, "call": 0.3, "first": 1.0, "wake": 0.15,
+       "rel": "V", "steps": "n0 s0 n1 s1 n2 f01 s2 n3 s3 f2 f3 c01 r0 c23 r1", "calls": CALLS, "last": CALLS}
 
 BF, F32, F16 = "bfloat16", "float32", "float16"
 SCRATCH = {k: ("sbuf", [128, n], d) for k, n, d in [
-    ("xs", NS * S, BF), ("tab", NS * TB, BF), ("gat", NS * C * 16, BF), ("snd", NS * RO * SW, BF), ("lnd", NS * RO * S, BF),
-    ("zpl", Z + NS * 128, BF), ("polb", NS * 128, BF), ("polh", NS * 128, F16), ("ones", 256, BF), ("eig", 256, BF),
-    ("kth", 128, BF), ("idn", 128, BF), ("zf", 2 * Z + W, BF), ("zsel", (2 * NCC - 1) * 64, BF), ("negr", TW, BF),
-    ("tri", 128, BF), ("creg", TW, BF), ("dmp", TW, F32), ("kmk", TW, BF), ("pidx", 8, "int32"), ("pq", 8, "int32"),
-    ("pqf", 8, F32), ("elc", 16, F32), ("els", 16, "uint16"), ("lqc", 240, F32), ("lq", 240, F16), ("cw", 256, BF),
-    ("off", NS * C, "uint16"), ("rel", NS * C, F16), ("vv", NS * C, BF), ("wr", NS * C, BF), ("uu", NS * TW, BF),
-    ("mb", NS * (3 * BW + TW), BF), ("scn", NS * TW, F32), ("ee", NS * TW, F16), ("pos", NS * KC, "uint16"),
-    ("yo", NS * C, BF)]}
-for _b in ("pnum", "ph0", "ph1", "pw0", "pw1", "pt0", "pt1", "pa"):
+    ("xs", S, BF), ("xl", S, BF), ("tab", NS * TB, BF), ("gat", NS * C * 16, BF), ("snd", NS * RO * SW, BF), ("lnd", NS * RO * S, BF),
+    ("plr", 3 * W, BF), ("zq", GAP + 2 * NS * (W + GAP), BF), ("polb", NS * 128, BF), ("polh", NS * 128, F16),
+    ("msk", 80, BF), ("ones", 384, BF), ("eig", 128, BF), ("idn", 128, BF), ("zf", 3 * W, BF), ("zsel", 128, BF), ("cst", 192, BF),
+    ("negr", 64, BF), ("key", 384, BF), ("tri", 384, BF), ("creg", 128, BF), ("dmp", 128, F32), ("pidx", 8, "int32"),
+    ("pq", 8, "int32"), ("pf", 8, F32), ("elc", 16, F32), ("els", 8, "uint16"), ("lqc", 240, F32), ("lq", 240, F16),
+    ("off", NS * C, "uint16"), ("rel", NS * C, F16), ("vv", NS * C, BF), ("wr", NS * C, BF),
+    ("mb", NS * 128, BF), ("scn", NS * 136, F32), ("ee", NS * 128, F16), ("pos", NS * 16, "uint16"), ("yo", NS * C, BF)]}
+for _b in ("pn0", "pn1", "ph0", "ph1", "pw0", "pw1", "pt", "pa"):
     SCRATCH[_b] = ("psum", [128, 512], F32)
 
-SEMAPHORES = ["eV", "eS", "eP", "eG", "sent"]
-SEMAPHORES += ["ar%d_%d_%d" % (s, t, b) for s in range(NS) for t in range(RO) for b in range(NB if t < RO - 1 else 1)]
-SEMAPHORES += ["d%d" % i for i in range(NS * (1 + 4 * NS))]
+SEMAPHORES = ["eV", "eS", "eP", "eG", "sent", "st"]
+SEMAPHORES += ["ar%d_%d_%d" % (s, t, b) for s in range(NS) for t in range(RO) for b in range(4)]
+SEMAPHORES += ["d%d" % i for i in range(6 * NS + 1)]
 
 
 def build(T, rank, core, topo, P):
@@ -56,196 +40,189 @@ def build(T, rank, core, topo, P):
     ndma = [0]
 
     def add(eng, fn, R, Wr, dur, **kw):
-        o = {"eng": eng, "fn": fn, "R": R, "W": Wr, "dur": dur, "i": len(ops), "s": 0, "fill": False}
+        o = {"eng": eng, "fn": fn, "R": R, "W": Wr, "dur": dur, "i": len(ops)}
         o.update(kw)
         ops.append(o)
 
-    def vec(fn, R, Wr, n, **kw):
-        add("V", fn, R, Wr, P["fix"] + max(64, n) * cyc, **kw)
+    def vec(fn, R, Wr, n, eng="V", **kw):
+        add(eng, fn, R, Wr, max(64, n) * cyc, **kw)
 
-    def gp(fn, R, Wr, n, base=0.15, **kw):
+    def gp(fn, R, Wr, n, base=0.17, **kw):
         add("G", fn, R, Wr, base + 2 * n * cyc, **kw)
 
-    def pe(mms, R, Wr, **kw):
-        def fn(q):
-            ins = None
-            for m in mms: ins = q.matmul(m[0], m[1], m[2], m[3], m[4])
-            return ins
-        add("P", fn, R, Wr, 0.02 + sum(max(64, m[5]) for m in mms) * P["pe"] * P["f"], **kw)
+    def pe(mms, R, Wr, step=None, **kw):
+        step = step or P["mm"]
+        for k in range(0, len(mms), step):
+            add("P", lambda q, part=mms[k:k + step]: [q.matmul(*m) for m in part][-1], R, Wr,
+                sum(max(64, m[2].shape[-1]) for m in mms[k:k + step]) * P["pe"] * P["f"], **kw)
 
     def dma(eng, out, in_, R, Wr, rows, nbytes, **kw):
-        ndma[0] += 1
-        add(eng, lambda q: q.dma_start(out, in_), R, Wr, 0.06, sem="d%d" % (ndma[0] - 1), rows=rows, nb=nbytes, **kw)
+        if "sem" not in kw:
+            ndma[0] += 1
+            kw["sem"] = "d%d" % (ndma[0] - 1)
+        add(eng, lambda q: q.dma_start(out, in_), R, Wr, 0.06, rows=rows, nb=nbytes, **kw)
 
-    vec(lambda q: q.memset(T.polb[:], 0.0), [], ["polz"], NS * 64)
-    for s in range(NS):
-        r0, r1 = s * W, (s + 1) * W
-        b0 = Z + s * 128
-        first = s == 0
-        dma("S" if first else "Y", T.xs[0:W, s * S:(s + 1) * S], T.x[r0:r1, :], [], ["xs%d" % s], W, 2 * S, order=10 * s)
-        dma("Y", T.zpl[0:W, b0:b0 + W], T.pl[r0:r1, r0:r1], [], ["zpl%d.0" % s], W, 2 * W, order=10 * s)
-        for i in range(NS):
-            dma("S" if first and i % 2 else "Y", T.tab[i * W:(i + 1) * W, s * TB + 16:(s + 1) * TB], T.lut[r0:r1, :], [],
-                ["tab%d.%d" % (s, i)], W, 2 * LW, order=10 * s + 1)
-        for i in range(NS):
-            dma("Y", T.polb[i * W:(i + 1) * W, s * 128 + i * W:s * 128 + (i + 1) * W], T.pol[r0:r1, r0:r1], ["polz"],
-                ["polb%d.%d" % (s, i)], W, 2 * W, order=10 * s + 2)
-    for s in range(NS):
-        for i in range(1, NS):
-            dma("Y", T.zpl[i * W:(i + 1) * W, Z + s * 128:Z + s * 128 + W], T.pl[s * W:(s + 1) * W, s * W:(s + 1) * W], [],
-                ["zpl%d.%d" % (s, i)], W, 2 * W, order=100 + s)
-
-    for k in range(NS + 1):
-        vec(lambda q, k=k: q.memset(T.zpl[:, k * 128:k * 128 + Z], 0.0), [], ["zplz%d" % k], Z // 2)
-    vec(lambda q: q.memset(T.ones[:], 1.0), [], ["ones"], 128)
-    vec(lambda q: q.memset(T.eig[:], 0.125), [], ["eig"], 128)
-    vec(lambda q: q.memset(T.kth[:], 1.0 / 1024), [], ["kth"], 64)
-    vec(lambda q: q.memset(T.cw[0:64, :], 0.0), [], ["cw"], 64)
-    vec(lambda q: q.memset(T.cw[0:1, 128:256], 0.5), [], ["cw"], 64)
-    vec(lambda q: q.memset(T.cw[0:1, 0:128], OFFS + 0.5), [], ["cw"], 64)
-    vec(lambda q: q.memset(T.cw[32:33, :], -2.0 ** -17), [], ["cw"], 64)
-    gp(lambda q: q.affine_select(T.idn[:], T.ones[:, 0:128], [[-1, 128]], ALU.is_equal, 0.0, 0, 1), ["ones"], ["idn"], 128)
-    vec(lambda q: q.memset(T.zf[:], 0.0), [], ["zf%d" % i for i in range(NS)], Z + W // 2)
-    for i in range(NS):
-        vec(lambda q, i=i: q.tensor_copy(T.zf[i * W:(i + 1) * W, Z:Z + W], T.idn[i * W:(i + 1) * W, i * W:(i + 1) * W]), ["idn"], ["zf%d" % i], 32)
-    sw, so = (2 * NCC - 1) * 8, 128 * (NCC - 1)
-    gp(lambda q: q.affine_select(T.zsel[:], T.eig[:, 0:sw * 8], [[-16, sw], [0, 8]], ALU.is_ge, 0.0, so, 1), ["eig"], ["zsel"], sw * 8)
-    gp(lambda q: q.affine_select(T.zsel[:], T.zsel[:], [[16, sw], [0, 8]], ALU.is_ge, 0.0, 15 - so, -1), ["zsel"], ["zsel"], sw * 8)
     flag = {"allow_small_or_imprecise_dtypes": True}
-    gp(lambda q: q.iota(T.negr[:], [[0, TW // 8], [-1, 8]], 0, 0, **flag), [], ["negr"], TW)
-    gp(lambda q: q.affine_select(T.tri[:], T.ones[:, 0:128], [[1, 128]], ALU.is_gt, 0.0, 0, -1), ["ones"], ["tri"], 128)
-    gp(lambda q: q.affine_select(T.tri[:], T.tri[:], [[1, 128]], ALU.not_equal, -8192.0, 0, -1), ["tri"], ["tri"], 128)
-    gp(lambda q: q.iota(T.creg[:], [[0, TW // 8], [4, 8]], 48, 0, **flag), [], ["creg"], TW)
-    gp(lambda q: q.iota(T.dmp[:], [[256, 4], [0, BW]], 2048, 2, **flag), [], ["dmp"], TW)
-    gp(lambda q: q.affine_select(T.dmp[:], T.dmp[:], [[0, TW // 8], [1, 8]], ALU.is_equal, -10000.0, 0, 0), ["dmp"], ["dmp"], TW)
-    gp(lambda q: q.affine_select(T.kmk[:], T.ones[:, 0:TW], [[0, TW // 8], [-16, 8]], ALU.is_ge, 0.0, 0, 1), ["ones"], ["kmk"], TW)
-    gp(lambda q: q.affine_select(T.kmk[:], T.kmk[:], [[0, TW // 8], [16, 8]], ALU.is_ge, 0.0, 15, -1), ["kmk"], ["kmk"], TW)
-    gp(lambda q: q.iota(T.pidx[:, 0:2], [[0, 2]], 0, 1), [], ["pidx"], 2)
-    ec = TW // 16
-    gp(lambda q: q.iota(T.elc[:, 0:ec], [[8 if NCC == 2 else 16, ec]], 7, 0, **flag), [], ["elc"], ec)
-    gp(lambda q: q.iota(T.lqc[:], [[1, 240]], -112, 0, **flag), [], ["lqc"], 240)
-    vec(lambda q: q.tensor_scalar(T.pq[:, 0:1], T.pidx[:, 0:1], 8, None, ALU.bitwise_and), ["pidx"], ["pq0"], 1)
-    vec(lambda q: q.tensor_scalar(T.pq[:, 1:2], T.pidx[:, 1:2], 15, None, ALU.bitwise_and), ["pidx"], ["pq1"], 1)
-    vec(lambda q: q.tensor_scalar(T.pqf[:, 0:1], T.pq[:, 0:1], 8.0 if NCC == 2 else 1.0, None, ALU.mult), ["pq0"], ["pqf0"], 1)
-    vec(lambda q: q.tensor_copy(T.pqf[:, 1:2], T.pq[:, 1:2]), ["pq1"], ["pqf1"], 1)
-    vec(lambda q: q.tensor_scalar(T.els[:, 0:ec], T.elc[:, 0:ec], T.pqf[:, 0:1], None, ALU.add), ["elc", "pqf0"], ["els"], ec)
-    vec(lambda q: q.tensor_scalar(T.lq[:], T.lqc[:], T.pqf[:, 1:2], None, ALU.is_equal), ["lqc", "pqf1"], ["lq"], 240)
-    mbw = 3 * BW + TW
-    for s in range(NS):
-        vec(lambda q, s=s: q.memset(T.mb[:, s * mbw:s * mbw + 3 * BW], 0.0), [], ["mbz%d" % s], 48, s=s)
-        vec(lambda q, s=s: q.memset(T.tab[:, s * TB:s * TB + 16], 0.0), [], ["tabz%d" % s], 8, s=s)
-        vec(lambda q, s=s: q.tensor_scalar(T.polh[:, s * 128:(s + 1) * 128], T.polb[:, s * 128:(s + 1) * 128], 2.0 ** -8, None, ALU.mult),
-            ["polz"] + ["polb%d.%d" % (s, i) for i in range(NS)], ["polh%d" % s], 64, s=s)
-    for t in range(RO):
-        for s in range(NS):
-            for r in range(N):
-                a = (s * RO + t) * SW + r * 512
-                gp(lambda q, a=a: q.iota(T.snd[:, a:a + CAP], [[0, CAP]], 0, 0, **flag), [], ["sz%d.%d.%d" % (s, t, r)], CAP,
-                   base=0.13, s=s, fill=True)
+    qb = lambda s, half: GAP + (2 * s + half) * (W + GAP)
 
-    zplz = ["zplz%d" % k for k in range(NS + 1)]
-    kb_own = blk_rel(rank)
-    cnt = [0]
+    def loads(s):
+        r0, r1 = s * W, (s + 1) * W
+        for i in range(2):
+            dma("Y", T.tab[i * W:(i + 1) * W, s * TB + 16:(s + 1) * TB], T.lut[r0:r1, :], [], ["tab%d.%d" % (s, i)], W, 2 * LW)
+        for i in range(2):
+            dma("Y", T.polb[i * W:(i + 1) * W, s * 128 + i * W:s * 128 + (i + 1) * W], T.pol[r0:r1, r0:r1], ["polz"],
+                ["polb%d.%d" % (s, i)], W, 2 * W)
 
-    def came(s, t, a):
+    def halves(s, i):
+        p, o = slice(i * W, (i + 1) * W), s * W if i == s else 128
+        for half in range(2):
+            vec(lambda q, half=half: q.tensor_tensor(T.zq[p, qb(s, half):qb(s, half) + W], T.plr[p, o:o + W], T.msk[p, 8 * half:8 * half + W], ALU.mult),
+                ["plr" if i == s else "plr%d" % s, "msk"], ["zq%d.%d.%d" % (s, half, i)], 2 * W)
+
+    def own_constants(s):
+        vec(lambda q: q.memset(T.scn[:, s * 136 + 128:s * 136 + 136], 0.0), [], ["scz%d" % s], 8)
+        vec(lambda q: q.memset(T.tab[:, s * TB:s * TB + 16], 0.0), [], ["tabz%d" % s], 8)
+        vec(lambda q: q.tensor_scalar(T.polh[:, s * 128:(s + 1) * 128], T.polb[:, s * 128:(s + 1) * 128], 2.0 ** -7, None, ALU.mult),
+            ["polz"] + ["polb%d.%d" % (s, i) for i in range(2)], ["polh%d" % s], 64)
+
+    def constants():
+        vec(lambda q: q.memset(T.ones[:], 1.0), [], ["ones"], 192)
+        vec(lambda q: q.memset(T.eig[:, 0:64], 0.125), [], ["eig0"], 64)
+        vec(lambda q: q.memset(T.eig[:, 64:128], -0.125), [], ["eig1"], 64)
+        for k, v in enumerate([-7.0 / 16, MAGIC, -MAGIC]):
+            vec(lambda q, k=k, v=v: q.memset(T.cst[0:1, k * 64:k * 64 + 64], v), [], ["cst%d" % k], 64)
+        gp(lambda q: q.iota(T.pidx[:, 0:1], [[0, 1]], 0, 1), [], ["pidx"], 2, base=0.13)
+        gp(lambda q: q.affine_select(T.idn[:], T.ones[:, 0:128], [[-1, 128]], ALU.is_equal, 0.0, 0, 1), ["ones"], ["idn"], 128)
+        vec(lambda q: q.memset(T.zf[:], 0.0), [], ["zf0", "zf1"], 96)
+        for i in range(2):
+            vec(lambda q, i=i: q.tensor_copy(T.zf[i * W:(i + 1) * W, W:2 * W], T.idn[i * W:(i + 1) * W, i * W:(i + 1) * W]), ["idn"], ["zf%d" % i], 32)
+        gp(lambda q: q.iota(T.key[:, 0:128], [[128, 2], [1, 32], [64, 2]], 0, 0, **flag), [], ["key0"], 128, base=0.13)
+        gp(lambda q: q.iota(T.key[:, 128:256], [[128, 2], [0, 32], [64, 2]], 64, 0, **flag), [], ["key1"], 128, base=0.13)
+        gp(lambda q: q.iota(T.key[:, 256:384], [[128, 2], [0, 32], [64, 2]], 0, 0, **flag), [], ["key2"], 128, base=0.13)
+        pe([[T.pa[:, 0:384], T.key[0:1, 0:128], T.ones[0:1, 0:384], True, True]], ["key0", "ones"], ["pa"])
+        vec(lambda q: q.tensor_tensor(T.tri[:], T.pa[:, 0:384], T.key[:], ALU.is_lt), ["key0", "key1", "key2"], ["pa", "tri"], 384)
+        gp(lambda q: q.iota(T.elc[:, 0:8], [[8, 8]], 7 - 128, 0, **flag), [], ["elc"], 8, base=0.13)
+        gp(lambda q: q.iota(T.lqc[:], [[1, 240]], -112, 0, **flag), [], ["lqc"], 240, base=0.13)
+        gp(lambda q: q.iota(T.negr[:], [[0, 8], [-1, 8]], 0, 0, **flag), [], ["negr"], 64, base=0.13)
+        vec(lambda q: q.tensor_scalar(T.negr[:], T.negr[:], 0.125, None, ALU.mult), ["negr"], ["negr"], 64)
+        gp(lambda q: q.affine_select(T.zsel[:], T.eig[:], [[0, 2], [-16, 8], [0, 8]], ALU.is_ge, 0.0, 0, 1), ["eig0", "eig1"], ["zsel"], 128)
+        gp(lambda q: q.affine_select(T.zsel[:], T.zsel[:], [[0, 2], [16, 8], [0, 8]], ALU.is_ge, 0.0, 15, -1), ["zsel"], ["zsel"], 128)
+        gp(lambda q: q.affine_select(T.tri[:, 0:128], T.tri[:, 0:128], [[1, 128]], ALU.not_equal, -8192.0, 0, -1), ["tri"], ["tri"], 128)
+        gp(lambda q: q.iota(T.creg[:], [[0, 16], [4, 8]], 48, 0, **flag), [], ["creg"], 128, base=0.13)
+        gp(lambda q: q.iota(T.dmp[:], [[256, 4], [0, 32]], 2048, 2, **flag), [], ["dmp"], 128, base=0.13)
+        gp(lambda q: q.affine_select(T.dmp[:], T.dmp[:], [[0, 16], [1, 8]], ALU.is_equal, -10000.0, 0, 0), ["dmp"], ["dmp"], 128)
+        for k, (op, v) in enumerate([(ALU.bitwise_and, 7), (ALU.bitwise_and, 8), (ALU.bitwise_and, 15), (ALU.arith_shift_right, 4)]):
+            vec(lambda q, k=k, op=op, v=v: q.tensor_scalar(T.pq[:, k:k + 1], T.pidx[:, 0:1], v, None, op), ["pidx"], ["pq%d" % k], 1)
+        vec(lambda q: q.tensor_tensor(T.pf[:, 0:1], T.pq[:, 0:1], T.pq[:, 3:4], ALU.is_equal), ["pq0", "pq3"], ["pf0"], 1)
+        vec(lambda q: q.tensor_scalar(T.pf[:, 1:2], T.pq[:, 1:2], 8.0, None, ALU.mult), ["pq1"], ["pf1"], 1)
+        vec(lambda q: q.tensor_copy(T.pf[:, 2:3], T.pq[:, 2:3]), ["pq2"], ["pf2"], 1)
+        vec(lambda q: q.tensor_scalar(T.elc[:, 8:16], T.elc[:, 0:8], T.pf[:, 1:2], T.pf[:, 0:1], ALU.add, ALU.mult), ["elc", "pf0", "pf1"], ["eld"], 8)
+        vec(lambda q: q.tensor_scalar(T.lq[:], T.lqc[:], T.pf[:, 2:3], None, ALU.is_equal), ["lqc", "pf2"], ["lq"], 240)
+        vec(lambda q: q.tensor_scalar(T.els[:], T.elc[:, 8:16], 128.0, None, ALU.add), ["eld"], ["els"], 8)
+
+    cnt = {"pn": 0, "ph": 0, "pw": 0}
+
+    def bank(k):
+        cnt[k] += 1
+        return "%s%d" % (k, cnt[k] % 2)
+
+    def came(s, t, a, lo=0, hi=CAP):
+        if t < 0: return T.xs[s * W:(s + 1) * W, a * CAP + lo:a * CAP + hi]
         if a == rank:
             o = (s * RO + t) * SW + rank * 512
-            return T.snd[:, o:o + CAP]
+            return T.snd[:, o + lo:o + hi]
         o = (s * RO + t) * S + a * CAP
-        return T.lnd[:, o:o + CAP]
+        return T.lnd[:, o + lo:o + hi]
 
     def ply(s, t):
-        c0 = s * C
-
-        def merged(out, kb, mat, m0, first, last):
-            mms = []
-            for i in range(NS):
-                a = 2 * ((kb // 2) * NS + i) + kb % 2
-                lo = m0 - i * W
-                if t == 0: mms.append([out, mat[0:W, lo:lo + 128], T.xs[0:W, s * S + a * CAP:s * S + (a + 1) * CAP], False, False, 64])
-                else: mms.append([out, mat[:, lo:lo + 128], came(s, t - 1, a), False, False, 64])
-            mms[0][3] = first
-            mms[-1][4] = last
-            return mms
-
-        def src(b):
-            if t == 0: return ["xs%d" % s], None
-            return ["snd%d.%d" % (s, t - 1)], (s, t - 1, b)
-
-        def span(ch):
-            return min(kb_own ^ b for b in ch) * 64, max(kb_own ^ b for b in ch) * 64 + 64
-
-        for grp in (NUMS if t else [[list(range(NB))]]):
-            for ch in grp:
-                for b in ch:
-                    kb = kb_own ^ b
-                    R, ext = src(b)
-                    zp = ["zpl%d.%d" % (s, i) for i in (range(NS) if t else [0])]
-                    pe(merged(T.pnum[:, kb * 64:kb * 64 + 64], kb, T.zpl, Z + s * 128, True, True), R + zp + zplz, ["pnum"], s=s, ext=ext)
-            for ch in grp:
-                lo, hi = span(ch)
-                vec(lambda q, lo=lo, hi=hi: q.tensor_scalar(T.off[:, c0 + lo:c0 + hi], T.pnum[:, lo:hi],
-                                                            16 - 273.0 * OFFS if t else 16.0, 0.0, ALU.add, ALU.max),
-                    [], ["pnum"] + ["off%d.%d" % (s, b) for b in ch], hi - lo, s=s)
-        ptn = "pt%d" % (s % 2)
-        pt = T[ptn]
-        pe([[pt[:, 0:TW], T.kth[:], T.negr[:], True, False, TW]], ["kth", "negr"], [ptn], s=s)
-        pe([[T.pa[:, 0:TW], T.ones[:, 0:128], T.creg[:], True, False, TW]], ["ones", "creg"], ["pa"], s=s)
-        done = []
-        for ch in CHUNKS:
-            hn, wn = "ph%d" % (cnt[0] % 2), "pw%d" % (cnt[0] % 2)
-            cnt[0] += 1
-            ph, pw = T[hn], T[wn]
-            lo, hi = span(ch)
-            for b in ch:
-                kb = kb_own ^ b
-                for u in range(64 // UC):
-                    add(("V", "S"), None, ["off%d.%d" % (s, b), "tabz%d" % s] + ["tab%d.%d" % (s, i) for i in range(NS)],
-                        ["gat%d.%d.%d" % (s, b, u)], UC * 16 * P["c"] * cyc, s=s, fill=True, gat=(s, t, b, u), col=c0 + kb * 64 + u * UC)
-                g0 = (c0 + kb * 64) * 16
-                for hf in range(2):
-                    pe([[ph[:, kb * 64:kb * 64 + 64], T.idn[:], T.gat[:, g0 + j:g0 + 1024:16], j == 0, j == 15, 64]
-                        for j in range(hf * 8, hf * 8 + 8)], ["idn"] + ["gat%d.%d.%d" % (s, b, u) for u in range(64 // UC)], [hn], s=s)
-            nm = "%d.%d" % (s, ch[0])
-            vec(lambda q, ph=ph, lo=lo, hi=hi: q.tensor_scalar(T.rel[:, c0 + lo:c0 + hi], ph[:, lo:hi], 0.0, 2.0 ** -8, ALU.max, ALU.mult),
-                [], [hn, "rel" + nm], hi - lo, s=s)
-            for b in ch:
-                kb = kb_own ^ b
-                R, ext = src(b)
-                o = pw[:, kb * 64:kb * 64 + 64]
-                pe([[o, T.cw[0:64, min(t, 1) * 128:min(t, 1) * 128 + 128], T.ones[0:64, 0:64], True, False, 64]]
-                   + merged(o, kb, T.zf, Z, False, False), R + ["cw", "ones"] + ["zf%d" % i for i in range(NS)], [wn], s=s, ext=ext)
-                pe([[o, T.polh[:, s * 128:(s + 1) * 128], T.rel[:, c0 + kb * 64:c0 + kb * 64 + 64], False, True, 64]],
-                   ["polh%d" % s, "rel" + nm], [wn], s=s)
-            vec(lambda q, pw=pw, lo=lo, hi=hi: q.tensor_scalar(T.vv[:, c0 + lo:c0 + hi], pw[:, lo:hi], MAGIC, MAGIC, ALU.add, ALU.subtract),
-                [], [wn, "vv" + nm], hi - lo, s=s)
-            before = len(done) // 2
-            done += ch
-            for cr in range(before, len(done) // 2):
-                cc = (kb_own // 2) ^ cr
-                z0 = (NCC - 1 - cc) * 64
-                pe([[pt[:, 0:TW], T.vv[:, c0 + cc * 128:c0 + cc * 128 + 128], T.zsel[:, z0:z0 + TW], False, cr == NCC - 1, TW]],
-                   ["zsel"] + ["vv%d.%d" % (s, x[0]) for x in CHUNKS if x[0] in done], [ptn], s=s)
-        vvs = ["vv%d.%d" % (s, x[0]) for x in CHUNKS]
-        t0, m0 = s * TW, s * mbw
-        vec(lambda q: q.tensor_scalar(T.wr[:, c0:c0 + C], T.vv[:, c0:c0 + C], OFFS + 16.0, -16.0, ALU.is_ge, ALU.mult), vvs, ["wr%d" % s], C // 2, s=s)
-        vec(lambda q: q.tensor_scalar(T.uu[:, t0:t0 + TW], pt[:, 0:TW], 128.0, None, ALU.max), [], [ptn, "uu%d" % s], TW, s=s)
-        vec(lambda q: q.tensor_tensor(T.mb[:, m0 + 3 * BW:m0 + mbw], pt[:, 0:TW], T.uu[:, t0:t0 + TW], ALU.is_equal),
-            ["uu%d" % s], [ptn, "mb%d" % s], TW, s=s)
-        pe([[T.pa[:, 0:TW], T.ones[:, 0:128] if j else T.tri[:], T.mb[:, m0 + (3 - j) * BW:m0 + (3 - j) * BW + TW], False, j == 3, TW]
-            for j in range(4)], ["mb%d" % s, "mbz%d" % s, "tri", "ones"], ["pa"], s=s)
-        vec(lambda q: q.tensor_tensor_scan(T.scn[:, t0:t0 + TW], T.dmp[:], T.pa[:, 0:TW], -10000.0, ALU.max, ALU.min),
-            ["dmp"], ["pa", "scn%d" % s], TW, s=s)
-        vec(lambda q: q.tensor_tensor(T.ee[:, t0:t0 + TW], T.scn[:, t0:t0 + TW].indirect(T.els[:, 0:ec]), T.kmk[:], ALU.mult),
-            ["scn%d" % s, "els", "kmk"], ["ee%d" % s], TW * max(2, P["c"]), s=s)
-        pe([[pt[:, 0:KC], T.lq[:, 112 - 16 * h:240 - 16 * h], T.ee[:, t0 + h * KC:t0 + (h + 1) * KC], h == 0, h == 7, KC] for h in range(8)],
-           ["lq", "ee%d" % s], [ptn], s=s)
-        vec(lambda q: q.tensor_scalar(T.pos[:, s * KC:(s + 1) * KC], pt[:, 0:KC], 2048.0, None, ALU.add), [], [ptn, "pos%d" % s], KC, s=s)
+        c0, t0 = s * C, s * 128
+        k0, k1 = (0, 128) if t else (s * W, (s + 1) * W)
         w0 = (s * RO + t) * SW
-        vec(lambda q: q.tensor_tensor(T.snd[:, w0:w0 + SW].indirect(T.pos[:, s * KC:(s + 1) * KC]), T.vv[:, c0:c0 + C], T.wr[:, c0:c0 + C], ALU.add),
-            vvs + ["wr%d" % s, "pos%d" % s] + ["sz%d.%d.%d" % (s, t, r) for r in range(N)], ["snd%d.%d" % (s, t)], C * P["sc"], s=s)
-        last = t == RO - 1
-        for call in (CALLS_LAST if last else CALLS):
+        for r in range(N):
+            gp(lambda q, a=w0 + r * 512: q.iota(T.snd[:, a:a + CAP], [[0, CAP]], 0, 0, **flag), [], ["sz%d.%d.%d" % (s, t, r)], CAP, base=0.13)
+        col = lambda u: ((rank // 2) ^ u) * 64
+        span = lambda us: (min(col(u) for u in us), max(col(u) for u in us) + 64)
+        pw = [bank("pw"), bank("pw")]
+        ph = {}
+        for step in P["steps"].split():
+            if step[0] == "f": ph.update(dict.fromkeys([int(x) for x in step[1:]], bank("ph")))
+
+        def sources(u):
+            R, ext = (["snd%d.%d" % (s, t - 1)], (s, t - 1, u)) if t else (["xs"], None)
+            return R, ext, [(i, e, came(s, t - 1, col(u) // 32 + e, 32 * i, 32 * i + 32)) for i in range(2) for e in range(2)]
+
+        def numbers(u):
+            R, ext, four = sources(u)
+            pn = bank("pn")
+            for half in range(2):
+                z = qb(s, half) + 8 * half
+                pe([[T[pn][:, half * 32:half * 32 + 32], T.zq[k0:k1, z - W * i - 8 * e:z - W * i - 8 * e + 128], src, k == 0, k == 3]
+                    for k, (i, e, src) in enumerate(four)], R + ["zq%d.%d.%d" % (s, half, i) for i in (range(2) if t else [s])], [pn], ext=ext)
+            o = c0 + col(u)
+            vec(lambda q: q.tensor_scalar(T.off[:, o:o + 64], T[pn][:, 0:64], 16 - 273.0 * OFFS, 0.0, ALU.add, ALU.max), [], [pn, "off%d.%d" % (s, u)], 64)
+
+        def sums(u):
+            R, ext, four = sources(u)
+            o = col(u) % 128
+            names = [["gat%d.%d.%d.%d" % (s, u, half, k) for k in range(32 // UC)] for half in range(2)]
+            for half in range(2):
+                for k in range(32 // UC):
+                    add("VS", None, ["off%d.%d" % (s, u), "tabz%d" % s, "tab%d.0" % s, "tab%d.1" % s], [names[half][k]],
+                        UC * 16 * P["c"] * cyc, gat=(s, t, u, half * (u in P["split"])), col=c0 + col(u) + half * 32 + k * UC)
+            pe([[T[pw[u // 2]][:, o + e:o + 64:2], T.zf[k0:k1, W - W * i:W - W * i + 128], src, k == 0 and u % 2 == 0, False]
+                for k, (i, e, src) in enumerate(four)], R + ["zf0", "zf1"], [pw[u // 2]], ext=ext)
+            for half in range(2):
+                g0 = (c0 + col(u) + half * 32) * 16
+                pe([[T[ph[u]][:, o:o + 64], T.idn[:], T.gat[:, g0 + j:g0 + 512:8], j == 0 and half == 0, j == 7 and half == 1]
+                    for j in range(8)], ["idn"] + (names[half] if u in P["split"] else names[0] + names[1]), [ph[u]])
+
+        def fire(us):
+            lo, hi = span(us)
+            b, o, n = ph[us[0]], lo % 128, hi - lo
+            if P["rel"] == "V":
+                vec(lambda q: q.tensor_scalar(T.rel[:, c0 + lo:c0 + hi], T[b][:, o:o + n], 0.0, 2.0 ** -8, ALU.max, ALU.mult), [], [b, "rel%d.%d" % (s, us[0])], n)
+            else:
+                vec(lambda q: q.activation(T.rel[:, c0 + lo:c0 + hi], T[b][:, o:o + n], ACT.Relu, scale=2.0 ** -8), [], [b, "rel%d.%d" % (s, us[0])], n, eng="S")
+            pe([[T[pw[us[0] // 2]][:, o:o + n], T.polh[:, t0:t0 + 128], T.rel[:, c0 + lo:c0 + hi], False, us[-1] % 2 == 1]],
+               ["polh%d" % s, "rel%d.%d" % (s, us[0])], [pw[us[0] // 2]])
+
+        def changed(us):
+            lo, hi = span(us)
+            b, o = pw[us[0] // 2], lo % 128
+            vec(lambda q: q.tensor_scalar(T.vv[:, c0 + lo:c0 + hi], T[b][:, o:o + hi - lo], HALF, 17.0 / 32, ALU.add, ALU.max),
+                [], [b] + ["vv%d.%d" % (s, u) for u in us], hi - lo)
+
+        def route(cr):
+            cc = (rank // 4) ^ cr
+            vs, m0, a0 = T.vv[:, c0 + cc * 128:c0 + cc * 128 + 128], t0 + cc * 64, cc * 64
+            out, one = T.pt[:, 0:64], T.ones[0:1, 0:128]
+            pe([[out, one, T.cst[0:1, 0:64], True, False]], ["ones", "cst0"], ["pt"])
+            pe([[out, vs, T.zsel[:, 0:64], False, False], [out, one, T.cst[0:1, 64:128], False, False], [out, one, T.cst[0:1, 128:192], False, False],
+                [out, vs, T.zsel[:, 64:128], False, True]], ["zsel", "cst1", "cst2", "vv%d.%d" % (s, 2 * cr), "vv%d.%d" % (s, 2 * cr + 1)], ["pt"], step=4)
+            vec(lambda q: q.tensor_tensor(T.mb[:, m0:m0 + 64], out, T.negr[:], ALU.is_equal), ["negr"], ["pt", "mb%d.%d" % (s, cr)], 64)
+            if cr == 0: pe([[T.pa[:, 0:128], T.ones[:, 0:128], T.creg[:], True, False]], ["ones", "creg"], ["pa"])
+            mms = [[T.pa[:, a0 + o:a0 + o + n], T.tri[:, k * 128:k * 128 + 128], T.mb[:, m0 + i:m0 + i + n], False, False]
+                   for k, o, i, n in [(0, 0, 0, 64), (1, 32, 0, 32), (2, 0, 32, 32)]]
+            if cc == 0: mms += [[T.pa[:, o:o + n], T.ones[:, 0:128], T.mb[:, m0 + i:m0 + i + n], False, False] for o, i, n in [(64, 0, 64), (64, 32, 32), (96, 0, 32)]]
+            mms[-1][4] = cr == 1
+            add("P", lambda q: [q.matmul(*m) for m in mms][-1], ["mb%d.%d" % (s, cr), "tri", "ones"], ["pa"], 384 * P["pe"] * P["f"])
+
+        for step in P["steps"].split():
+            us = [int(x) for x in step[1:]]
+            {"n": numbers, "s": sums, "r": route, "f": fire, "c": changed}[step[0]](us if step[0] in "fc" else us[0])
+        vvs = ["vv%d.%d" % (s, u) for u in range(4)]
+        z0 = s * 136
+        vec(lambda q: q.tensor_tensor_scan(T.scn[:, z0:z0 + 128], T.dmp[:], T.pa[:, 0:128], -10000.0, ALU.max, ALU.min),
+            ["dmp"], ["pa", "scn%d" % s], 128)
+        vec(lambda q: q.tensor_copy(T.ee[:, t0:t0 + 128], T.scn[:, z0:z0 + 136].indirect(T.els[:])),
+            ["scn%d" % s, "scz%d" % s, "els"], ["ee%d" % s], 60 + 128 * P["c"])
+        pe([[T.pa[:, 0:16], T.lq[:, 112 - 16 * h:240 - 16 * h], T.ee[:, t0 + h * 16:t0 + (h + 1) * 16], h == 0, h == 7] for h in range(8)],
+           ["lq", "ee%d" % s], ["pa"], step=8)
+        vec(lambda q: q.tensor_scalar(T.pos[:, s * 16:(s + 1) * 16], T.pa[:, 0:16], 2048.0, None, ALU.add), [], ["pa", "pos%d" % s], 16)
+        vec(lambda q: q.tensor_scalar(T.wr[:, c0:c0 + C], T.vv[:, c0:c0 + C], OFFS + 16.0, -16.0, ALU.is_ge, ALU.mult), vvs, ["wr%d" % s], 128)
+        vec(lambda q: q.tensor_tensor(T.snd[:, w0:w0 + SW].indirect(T.pos[:, s * 16:(s + 1) * 16]), T.vv[:, c0:c0 + C], T.wr[:, c0:c0 + C], ALU.add),
+            vvs + ["wr%d" % s, "pos%d" % s] + ["sz%d.%d.%d" % (s, t, r) for r in range(N)], ["snd%d.%d" % (s, t)], 60 + C * P["sc"])
+        for call in P["last" if t == RO - 1 else "calls"]:
             def send(q, call=call):
                 trs, e0 = [], 0
                 for rel, ne in call:
@@ -256,36 +233,50 @@ def build(T, rank, core, topo, P):
                     o = w0 + (rank ^ rel) * 512
                     lo = (s * RO + t) * S + rank * CAP
                     trs.append(RemoteDMATransfer(dst_ids=[DstId(rid=rid, pnc=pid)], dma_engine_mask=sum(1 << e for e in eng),
-                                                 remote_sem=T.sem["ar%d_%d_%d" % (s, t, 0 if last else blk_rel(rel))],
+                                                 remote_sem=T.sem["ar%d_%d_%d" % (s, t, rel // 2)],
                                                  src=T.snd[:, o:o + CAP], dst=T.lnd[:, lo:lo + CAP]))
                 return q.remote_dma_fused(trs, local_sem=T.sem.sent)
-            add("G", send, ["snd%d.%d" % (s, t)], [], P["call"], s=s, call=call, st=(s, t))
+            add("G", send, ["snd%d.%d" % (s, t)], [], P["call"], call=call, st=(s, t))
 
+    def last(s):
+        for cr in range(2):
+            cc = (rank // 4) ^ cr
+            pn = bank("pn")
+            for u in (2 * cr, 2 * cr + 1):
+                i = ((rank // 2) ^ u) % 2
+                pe([[T[pn][i * W:(i + 1) * W, e * 64:e * 64 + 64], T.zf[:, W:2 * W], came(s, RO - 1, 4 * cc + 2 * i + e), True, True]
+                    for e in range(2)], ["snd%d.%d" % (s, RO - 1)], [pn], ext=(s, RO - 1, u))
+            o = s * C + cc * 128
+            vec(lambda q, pn=pn, o=o: q.tensor_scalar(T.yo[:, o:o + 128], T[pn][:, 0:128], -float(OFFS), -1.0, ALU.add, ALU.max),
+                [], [pn, "yo%d.%d" % (s, cr)], 128)
+            for i in range(2):
+                a = (4 * cc + 2 * i) * CAP
+                dma("YS"[i], T.y[s * W:(s + 1) * W, a:a + 128], T.yo[i * W:(i + 1) * W, o:o + 128], ["yo%d.%d" % (s, cr)], [], W, 256, sem="st")
+
+    vec(lambda q: q.memset(T.polb[:], 0.0), [], ["polz"], NS * 64)
+    vec(lambda q: q.memset(T.zq[:], 0.0), [], ["zq%d.%d.%d" % (s, h, i) for s in range(NS) for h in range(2) for i in range(2)], T.zq.shape[1] // 2)
+    gp(lambda q: q.iota(T.msk[:], [[0, 5], [-1, 2], [0, 8]], 1, 0, **flag), [], ["msk"], 80, base=0.13)
+    dma("S", T.xs[:], T.x[:], [], ["xs"], 128, 2 * S)
+    dma("Y", T.plr[:, 0:128], T.pl[:], [], ["plr"], 128, 256)
+    for s in range(NS): loads(s)
+    for s in range(NS):
+        dma("Y", T.plr[(1 - s) * W:(2 - s) * W, 128:128 + W], T.pl[s * W:(s + 1) * W, s * W:(s + 1) * W], [], ["plr%d" % s], W, 2 * W)
+    vec(lambda q: q.tensor_scalar(T.xl[:], T.xs[:], 0.0, float(OFFS), ALU.is_ge, ALU.mult), ["xs"], ["xl"], S // 2)
+    vec(lambda q: q.tensor_tensor(T.xs[:], T.xs[:], T.xl[:], ALU.add), ["xl"], ["xs"], 2 * S)
+    for s in range(NS): halves(s, s)
+    own_constants(0)
+    constants()
     for t in range(RO):
         for s in range(NS):
+            if s and not t: own_constants(s)
+            if t == 1: halves(s, 1 - s)
             ply(s, t)
-
-    for s in range(NS):
-        mms = []
-        for kb in range(NB):
-            for i in range(NS):
-                mms.append([T.pnum[:, kb * 64:kb * 64 + 64], T.zf[:, Z - i * W:Z - i * W + 128], came(s, RO - 1, i * NB + kb), i == 0, i == NS - 1, 64])
-        pe(mms, ["snd%d.%d" % (s, RO - 1)], ["pnum"], s=s, ext=(s, RO - 1, 0))
-        vec(lambda q, s=s: q.tensor_scalar(T.yo[:, s * C:(s + 1) * C], T.pnum[:, 0:C], -float(OFFS), -1.0, ALU.add, ALU.max),
-            [], ["pnum", "yo%d" % s], C, s=s)
-        for i in range(NS):
-            dma("S" if s == NS - 1 and i % 2 else "Y", T.y[s * W:(s + 1) * W, i * C:(i + 1) * C], T.yo[i * W:(i + 1) * W, s * C:(s + 1) * C],
-                ["yo%d" % s], [], W, 2 * C, order=1000 + s, s=s, store=True)
+    for s in range(NS): last(s)
     return ops
 
 
-def arrive_count(t, b):
-    last = t == RO - 1
-    return sum(ne for call in (CALLS_LAST if last else CALLS) for rel, ne in call if last or blk_rel(rel) == b)
-
-
 def depend(ops):
-    lastw, readers, sends = {}, {}, {}
+    lastw, readers, lastd = {}, {}, {}
     for o in ops:
         d = set()
         for r in o["R"]:
@@ -299,123 +290,58 @@ def depend(ops):
             readers[w] = []
         d.discard(o["i"])
         o["deps"] = sorted(d)
-        if "call" in o: sends.setdefault(o["st"], []).append(o["i"])
-        o["xd"] = sends[o["ext"][0:2]] if o.get("ext") else []
-    dm = sorted((o["order"], o["i"]) for o in ops if "sem" in o)
-    for q in ("Y", "S"):
-        seq = [i for _, i in dm if ops[i]["eng"] == q]
-        for a, b in zip(seq, seq[1:]): ops[b]["after"] = a
+        if "sem" in o or "call" in o:
+            o["after"] = lastd.get(o["eng"])
+            lastd[o["eng"]] = o["i"]
 
 
-def timing(ops, P):
-    fin, eng_of, arr = {}, {}, {}
-    free = {e: 0.0 for e in "VSPGY"}
-    st = {"first": True, "eng": [0.0] * 16, "prev": {}}
+def joins(p, o):
+    return "gat" in p and p["gat"] == o["gat"] and abs(p["col"] - o["col"]) == UC
 
-    def ready(o, e):
-        t = 0.0
-        for d in o["deps"]:
-            t = max(t, fin[d] + (0.0 if eng_of[d] == e == "P" else P["wake"] if "sem" in ops[d] else P["lat"]))
-        if o["xd"]: t = max(t, arr[o["ext"]] + P["wake"])
-        return t
 
-    def length(o, e):
-        if "gat" not in o: return o["dur"]
-        p = st["prev"].get(e)
-        joined = p is not None and "gat" in p and p["gat"][0:3] == o["gat"][0:3] and abs(p["gat"][3] - o["gat"][3]) == 1
-        return o["dur"] + (0.0 if joined else 0.06)
-
-    def commit(o, e, t):
-        d = length(o, e)
-        free[e] = t + d
-        fin[o["i"]] = t + d
-        eng_of[o["i"]] = e
-        st["prev"][e] = o
+def place(ops, P, order=None):
+    fin, arr, start, on = {}, {}, {}, {}
+    busy = {e: [] for e in "VSPGY"}
+    eng, first, pool = [0.0] * 16, P["first"], {}
+    for o in ops:
+        if "gat" in o: pool.setdefault(o["gat"], []).append(o)
+    for i, es in order or [(o["i"], o["eng"]) for o in ops]:
+        best = None
+        for e in es:
+            o = ops[i] if len(es) == 1 else pool[ops[i]["gat"]][0 if e == "S" else -1]
+            d, t = o["dur"], 0.0
+            for k in o["deps"]:
+                t = max(t, fin[k] + (0.0 if on[k] == e == "P" else P["wake"] if "sem" in ops[k] else P["lat"]))
+            if o.get("ext"): t = max(t, arr[o["ext"]] + P["wake"])
+            if o.get("after") is not None: t = max(t, start[o["after"]] + 1e-3)
+            b = busy[e]
+            k = len(b)
+            while not order and k and b[k - 1][1] > t: k -= 1
+            while True:
+                if k: t = max(t, b[k - 1][1])
+                new = "gat" in o and not (k and t == b[k - 1][1] and joins(ops[b[k - 1][2]], o))
+                if k == len(b) or t + d + 0.06 * new + P["room"] * ("gat" in o) <= b[k][0]: break
+                k += 1
+            x = t + d + 0.06 * new
+            cost = x + P["join"] * new + P["lean"] * (e == "V")
+            if best is None or cost < best[0]: best = (cost, e, k, t, x, o)
+        _, e, k, t, x, o = best
+        i = o["i"]
+        if len(es) > 1: pool[o["gat"]].remove(o)
+        busy[e].insert(k, (t, x, i))
+        start[i], fin[i], on[i] = t, x, e
         if "sem" in o:
-            b = max([t + P["dma0"]] + st["eng"]) + max(1, o["rows"] / 16) * (P["row"] + o["nb"] / P["bw"])
-            st["eng"] = [b] * 16
-            fin[o["i"]] = b
+            fin[i] = max([t + P["dma0"]] + eng * (o["sem"] != "st")) + o["rows"] / 16 * (P["row"] + o["nb"] / P["bw"])
+            if o["sem"] != "st": eng = [fin[i]] * 16
         if "call" in o:
-            t0 = t + d + P["dma0"] + (P["first"] if st["first"] else 0.0)
-            st["first"] = False
-            e0 = 0
+            t0, e0, first = x + P["dma0"] + first, 0, 0.0
             for rel, ne in o["call"]:
-                b = max([t0] + st["eng"][e0:e0 + ne]) + 128 / ne * (P["row"] + 128 / P["bw"])
-                for k in range(e0, e0 + ne): st["eng"][k] = b
+                x = max([t0] + eng[e0:e0 + ne]) + 128 / ne * (P["row"] + 128 / P["bw"])
+                eng[e0:e0 + ne] = [x] * ne
                 e0 += ne
-                key = o["st"] + (0 if o["st"][1] == RO - 1 else blk_rel(rel),)
-                arr[key] = max(arr.get(key, 0.0), b)
-    return ready, length, commit, free, fin
-
-
-def schedule(ops, P):
-    n = len(ops)
-    succ = [[] for _ in ops]
-    for o in ops:
-        for d in o["deps"]: succ[d].append((o["i"], P["lat"] + (P["dma0"] + o["dur"] if "sem" in ops[d] else 0.0)))
-        for d in o["xd"]: succ[d].append((o["i"], P["dma0"] + 1.0 + 0.4 * o["ext"][2]))
-    lev = [0.0] * n
-    for i in range(n - 1, -1, -1):
-        lev[i] = ops[i]["dur"] + max([lev[j] + x for j, x in succ[i]] + [0.0])
-    for o in ops:
-        lev[o["i"]] -= P["bias"] * o["s"] * 2 / NS
-        if "gat" in o: lev[o["i"]] -= P["gb"] * o["gat"][2] + P["g0"]
-        elif o["W"]: lev[o["i"]] += P["pri"].get(o["W"][-1].rstrip("0123456789."), 0.0)
-    ready, length, commit, free, fin = timing(ops, P)
-    need = lambda o: o["deps"] + o["xd"] + ([o["after"]] if "after" in o else [])
-    left = set(range(n))
-    order = []
-    while left:
-        rdy = [ops[i] for i in sorted(left) if all(d not in left for d in need(ops[i]))]
-        isr = set(o["i"] for o in rdy)
-        memo = {}
-
-        def soon(o, e, depth):
-            if o["i"] in isr: return max(ready(o, e), free[e])
-            if depth == 0 or o["xd"] and any(d in left for d in o["xd"]): return None
-            key = o["i"]
-            if key in memo: return memo[key]
-            t = 0.0
-            for d in need(o):
-                if d not in left:
-                    t = max(t, fin[d] + P["lat"])
-                    continue
-                p = ops[d]
-                x = None if p["fill"] or p["eng"] != "P" else soon(p, "P", depth - 1)
-                if x is None:
-                    t = None
-                    break
-                t = max(t, x + p["dur"] + (P["lat"] if e != "P" else 0.0))
-            memo[key] = t
-            return t
-
-        best, forced = None, None
-        for e in "PVSGY":
-            cand = [(max(ready(o, e), free[e]), o) for o in rdy if e in o["eng"]]
-            if not cand: continue
-            t0 = min(c[0] for c in cand)
-            now = [c for c in cand if c[0] <= t0 + 0.001]
-            sgn = 1 if e == "V" else -1
-            t, o = max(now, key=lambda c: (round(lev[c[1]["i"]], 3), sgn * c[1]["i"]))
-            end = t + length(o, e)
-            better = [c for c in cand if lev[c[1]["i"]] > lev[o["i"]] + 0.001 and not c[1]["fill"] and c[0] + P["theta"] < end]
-            if better: t, o = min(better, key=lambda c: c[0])
-            wait = False
-            if e == "V" and o["fill"]:
-                for i in left:
-                    p = ops[i]
-                    if p["eng"] == "V" and i not in isr and not p["fill"] and lev[i] > lev[o["i"]]:
-                        x = soon(p, "V", 3)
-                        if x is not None and x + P["theta"] < end:
-                            wait = True
-                            break
-            if forced is None or t < forced[0]: forced = (t, o, e)
-            if not wait and (best is None or t < best[0]): best = (t, o, e)
-        t, o, e = best or forced
-        commit(o, e, t)
-        left.discard(o["i"])
-        order.append((o["i"], e))
-    return order, max(fin.values())
+                key = o["st"] + (rel // 2,)
+                arr[key] = max(arr.get(key, 0.0), x)
+    return [(i, on[i]) for i in sorted(start, key=lambda i: (start[i], i))], max(fin.values()), busy
 
 
 PLAN = {}
@@ -427,13 +353,12 @@ def rank_program(g, core, T, topo):
         return
     ops = build(T, rank, core, topo, PAR)
     depend(ops)
-    if "order" not in PLAN: PLAN["order"] = schedule(ops, PAR)[0]
+    if "order" not in PLAN: PLAN["order"] = place(ops, PAR)[0]
     queues = {"V": g.vector, "S": g.scalar, "P": g.tensor, "G": g, "Y": g.sync}
     items, item_of, lastq = [], {}, {}
     for i, e in PLAN["order"]:
         o, p = ops[i], lastq.get(e)
-        if "gat" in o and p is not None and "gat" in p["ops"][-1] and p["ops"][-1]["gat"][0:3] == o["gat"][0:3] \
-                and abs(p["ops"][-1]["gat"][3] - o["gat"][3]) == 1 and all(d in p["deps"] or d in p["seen"] for d in o["deps"]):
+        if "gat" in o and p is not None and joins(p["ops"][-1], o) and all(d in p["deps"] or d in p["seen"] for d in o["deps"]):
             p["ops"].append(o)
         else:
             p = {"ops": [o], "e": e, "k": len(items), "deps": set(o["deps"]), "seen": set(item_of), "inc": False}
@@ -459,12 +384,13 @@ def rank_program(g, core, T, topo):
         p["waits"] = waits
         p["clock"] = dict(kn)
     count = {e: 0 for e in queues}
-    sent = 0
+    sent, stores = 0, 0
     for p in items:
         e, q, o = p["e"], queues[p["e"]], p["ops"][0]
         for w in p["waits"]:
             if "ext" in w:
-                q.wait_ge(T.sem["ar%d_%d_%d" % w["ext"]], arrive_count(w["ext"][1], w["ext"][2]))
+                s, t, u = w["ext"]
+                q.wait_ge(T.sem["ar%d_%d_%d" % (s, t, u)], sum(ne for call in PAR["last" if t == RO - 1 else "calls"] for rel, ne in call if rel // 2 == u))
             elif "sem" in w["ops"][0]:
                 q.wait_ge(T.sem[w["ops"][0]["sem"]], 16)
             else:
@@ -480,6 +406,7 @@ def rank_program(g, core, T, topo):
             ins = o["fn"](q)
         if "sem" in o:
             ins.then_inc(T.sem[o["sem"]], 16)
+            stores += 16 * (o["sem"] == "st")
         elif "call" in o:
             sent += sum(ne for rel, ne in o["call"])
         elif p["inc"]:
@@ -487,5 +414,4 @@ def rank_program(g, core, T, topo):
             p["n"] = count[e]
             ins.then_inc(T.sem["e" + e], 1)
     g.wait_ge(T.sem.sent, sent)
-    for o in ops:
-        if o.get("store"): queues[o["eng"]].wait_ge(T.sem[o["sem"]], 16)
+    g.sync.wait_ge(T.sem.st, stores)

@@ -10,19 +10,20 @@ TB = LW + 16
 GAP = 72
 OFFS = 132
 HALF = 0.5 - 2.0 ** -16
-MAGIC = 12582912.0
 UC = 4
-CALLS = [[(1, 16)], [(2, 8), (3, 8)], [(4, 8), (5, 8)], [(6, 8), (7, 8)]]
-PAR = {"c": 1.56, "sc": 3.8, "f": 1.0, "pe": 0.00042, "lat": 0.2, "room": 0.0, "join": 0.1, "lean": 0.0, "mm": 2, "split": [3],
-       "row": 0.03, "bw": 20000.0, "dma0": 1.0, "call": 0.3, "first": 1.0, "wake": 0.15,
-       "rel": "V", "steps": "n0 s0 n1 s1 n2 f01 s2 n3 s3 f2 f3 c01 r0 c23 r1", "calls": CALLS, "last": CALLS}
+PAR = {"c": 1.56, "sc": 3.8, "f": 1.0, "pe": 0.00042, "lat": 0.2, "join": 0.0, "mm": 1,
+       "row": 0.03, "bw": 20000.0, "dma0": 1.0, "call": 0.3, "first": 1.0, "wake": 0.15, "rel": "V", "vv": "VS", "lean": 0.0,
+       "polat": 0, "pad": {}, "cuts": [(0, 0, 2), (0, 2, 4), (0, 4, 8), (1, 4, 8)],
+       "steps": ["n1 n0 K | n3 s0 n2 p0 s1 s2 f01 c01 s3 f2 f3 r0 c23 r1 | q0", "n2 n0 n1 s0 n3 | s1 | p1 s2 f01 s3 c01 r0 f2 f3 c23 r1 q0",
+                 "| n0 n1 s0 n2 s1 s2 n3 f01 s3 c01 f2 r0 f3 c23 r1 q0 |", "n0 n1 n2 s0 n3 s1 s2 f01 s3 | f2 f3 c01 | c23 r0 r1 q0",
+                 "n0 n1 | n2 s0 n3 s1 s2 f01 c01 s3 r0 f2 f3 c23 r1 | q0", "n0 n1 s0 n3 s1 n2 f01 s2 s3 c01 | | f2 f3 r0 c23 r1 q0"]}
 
 BF, F32, F16 = "bfloat16", "float32", "float16"
 SCRATCH = {k: ("sbuf", [128, n], d) for k, n, d in [
     ("xs", S, BF), ("xl", S, BF), ("tab", NS * TB, BF), ("gat", NS * C * 16, BF), ("snd", NS * RO * SW, BF), ("lnd", NS * RO * S, BF),
-    ("plr", 3 * W, BF), ("zq", GAP + 2 * NS * (W + GAP), BF), ("polb", NS * 128, BF), ("polh", NS * 128, F16),
-    ("msk", 80, BF), ("ones", 384, BF), ("eig", 128, BF), ("idn", 128, BF), ("zf", 3 * W, BF), ("zsel", 128, BF), ("cst", 192, BF),
-    ("negr", 64, BF), ("key", 384, BF), ("tri", 384, BF), ("creg", 128, BF), ("dmp", 128, F32), ("pidx", 8, "int32"),
+    ("plr", 128, BF), ("zq", GAP + 3 * NS * (W + GAP), BF), ("polr", 128, BF), ("polh", NS * 128, F16),
+    ("msk", 80, BF), ("ones", 128, BF), ("eig", 256, BF), ("idn", 128, BF), ("zf", 3 * W, BF), ("zsel", 256, BF), ("cst", 64, BF),
+    ("negr", 64, BF), ("tri", 384, BF), ("creg", 128, BF), ("dmp", 128, F32), ("pidx", 8, "int32"),
     ("pq", 8, "int32"), ("pf", 8, F32), ("elc", 16, F32), ("els", 8, "uint16"), ("lqc", 240, F32), ("lq", 240, F16),
     ("off", NS * C, "uint16"), ("rel", NS * C, F16), ("vv", NS * C, BF), ("wr", NS * C, BF),
     ("mb", NS * 128, BF), ("scn", NS * 136, F32), ("ee", NS * 128, F16), ("pos", NS * 16, "uint16"), ("yo", NS * C, BF)]}
@@ -31,7 +32,7 @@ for _b in ("pn0", "pn1", "ph0", "ph1", "pw0", "pw1", "pt", "pa"):
 
 SEMAPHORES = ["eV", "eS", "eP", "eG", "sent", "st"]
 SEMAPHORES += ["ar%d_%d_%d" % (s, t, b) for s in range(NS) for t in range(RO) for b in range(4)]
-SEMAPHORES += ["d%d" % i for i in range(6 * NS + 1)]
+SEMAPHORES += ["d%d" % i for i in range(12)]
 
 
 def build(T, rank, core, topo, P):
@@ -63,54 +64,71 @@ def build(T, rank, core, topo, P):
         add(eng, lambda q: q.dma_start(out, in_), R, Wr, 0.06, rows=rows, nb=nbytes, **kw)
 
     flag = {"allow_small_or_imprecise_dtypes": True}
-    qb = lambda s, half: GAP + (2 * s + half) * (W + GAP)
+    qb = lambda s, half: GAP + (3 * s + half) * (W + GAP)
+    cnt = {"pn": 0, "ph": 0}
 
-    def loads(s):
-        r0, r1 = s * W, (s + 1) * W
-        for i in range(2):
-            dma("Y", T.tab[i * W:(i + 1) * W, s * TB + 16:(s + 1) * TB], T.lut[r0:r1, :], [], ["tab%d.%d" % (s, i)], W, 2 * LW)
-        for i in range(2):
-            dma("Y", T.polb[i * W:(i + 1) * W, s * 128 + i * W:s * 128 + (i + 1) * W], T.pol[r0:r1, r0:r1], ["polz"],
-                ["polb%d.%d" % (s, i)], W, 2 * W)
+    def bank(k):
+        cnt[k] += 1
+        return "%s%d" % (k, cnt[k] % 2)
 
-    def halves(s, i):
-        p, o = slice(i * W, (i + 1) * W), s * W if i == s else 128
+    def tables(s):
+        for i, lo, hi in P["cuts"] if s == 0 else [(0, 0, 8), (1, 0, 8)]:
+            dma("Y", T.tab[i * W:(i + 1) * W, s * TB + 16 + lo * 512:s * TB + 16 + hi * 512], T.lut[s * W:(s + 1) * W, lo * 512:hi * 512], [],
+                ["tab%d.%d.%d" % (s, i, k) for k in range(lo, hi)], W, 1024 * (hi - lo))
+
+    def copies():
+        for k in range(min([lo for i, lo, hi in P["cuts"] if i] + [8])):
+            b, o = ["pw0", "pw1", "pt", "pa"][k % 4], 16 + k * 512
+            pe([[T[b][W:128, :], T.idn[0:W, 0:W], T.tab[0:W, o:o + 512], True, True]], ["idn", "tab0.0.%d" % k], [b])
+            if k % 2: vec(lambda q, b=b, o=o: q.tensor_copy(T.tab[W:128, o:o + 512], T[b][W:128, :]), [], [b, "tab0.1.%d" % k], 512)
+            else: vec(lambda q, b=b, o=o: q.activation(T.tab[W:128, o:o + 512], T[b][W:128, :], ACT.Copy), [], [b, "tab0.1.%d" % k], 512, eng="S")
+
+    def placements(s):
+        p, b = slice(s * W, (s + 1) * W), bank("ph")
+        pe([[T[b][:, 0:W], T.zf[p, W - W * i:W - W * i + 128], T.plr[p, p], i == 0, i == 1] for i in range(2)], ["plr", "zf0", "zf1"], [b])
+        vec(lambda q: q.tensor_copy(T.zq[:, qb(s, 2):qb(s, 2) + W], T[b][:, 0:W]), [], [b, "zq%d.2" % s], W)
         for half in range(2):
-            vec(lambda q, half=half: q.tensor_tensor(T.zq[p, qb(s, half):qb(s, half) + W], T.plr[p, o:o + W], T.msk[p, 8 * half:8 * half + W], ALU.mult),
-                ["plr" if i == s else "plr%d" % s, "msk"], ["zq%d.%d.%d" % (s, half, i)], 2 * W)
-
-    def own_constants(s):
-        vec(lambda q: q.memset(T.scn[:, s * 136 + 128:s * 136 + 136], 0.0), [], ["scz%d" % s], 8)
+            vec(lambda q, half=half: q.tensor_tensor(T.zq[:, qb(s, half):qb(s, half) + W], T[b][:, 0:W], T.msk[:, 8 * half:8 * half + W], ALU.mult),
+                ["msk"], [b, "zq%d.%d" % (s, half)], W)
         vec(lambda q: q.memset(T.tab[:, s * TB:s * TB + 16], 0.0), [], ["tabz%d" % s], 8)
-        vec(lambda q: q.tensor_scalar(T.polh[:, s * 128:(s + 1) * 128], T.polb[:, s * 128:(s + 1) * 128], 2.0 ** -7, None, ALU.mult),
-            ["polz"] + ["polb%d.%d" % (s, i) for i in range(2)], ["polh%d" % s], 64)
 
-    def constants():
-        vec(lambda q: q.memset(T.ones[:], 1.0), [], ["ones"], 192)
-        vec(lambda q: q.memset(T.eig[:, 0:64], 0.125), [], ["eig0"], 64)
-        vec(lambda q: q.memset(T.eig[:, 64:128], -0.125), [], ["eig1"], 64)
-        for k, v in enumerate([-7.0 / 16, MAGIC, -MAGIC]):
-            vec(lambda q, k=k, v=v: q.memset(T.cst[0:1, k * 64:k * 64 + 64], v), [], ["cst%d" % k], 64)
-        gp(lambda q: q.iota(T.pidx[:, 0:1], [[0, 1]], 0, 1), [], ["pidx"], 2, base=0.13)
+    def policy(s):
+        p, b = slice(s * W, (s + 1) * W), bank("pn")
+        pe([[T[b][:, i * W:(i + 1) * W], T.zf[p, W - W * i:W - W * i + 128], T.polr[p, p], True, True] for i in range(2)], ["polr", "zf0", "zf1"], [b])
+        vec(lambda q: q.tensor_scalar(T.polh[:, s * 128:(s + 1) * 128], T[b][:, 0:128], 2.0 ** -7, None, ALU.mult), [], [b, "polh%d" % s], 128)
+
+    def first_constants():
+        vec(lambda q: q.memset(T.ones[:], 1.0), [], ["ones"], 64)
         gp(lambda q: q.affine_select(T.idn[:], T.ones[:, 0:128], [[-1, 128]], ALU.is_equal, 0.0, 0, 1), ["ones"], ["idn"], 128)
+        gp(lambda q: q.iota(T.msk[:], [[0, 5], [-1, 2], [0, 8]], 1, 0, **flag), [], ["msk"], 80, base=0.13)
         vec(lambda q: q.memset(T.zf[:], 0.0), [], ["zf0", "zf1"], 96)
+        vec(lambda q: q.memset(T.zq[:], 0.0), [], ["zq%d.%d" % (s, h) for s in range(NS) for h in range(3)], T.zq.shape[1] // 2)
         for i in range(2):
             vec(lambda q, i=i: q.tensor_copy(T.zf[i * W:(i + 1) * W, W:2 * W], T.idn[i * W:(i + 1) * W, i * W:(i + 1) * W]), ["idn"], ["zf%d" % i], 32)
-        gp(lambda q: q.iota(T.key[:, 0:128], [[128, 2], [1, 32], [64, 2]], 0, 0, **flag), [], ["key0"], 128, base=0.13)
-        gp(lambda q: q.iota(T.key[:, 128:256], [[128, 2], [0, 32], [64, 2]], 64, 0, **flag), [], ["key1"], 128, base=0.13)
-        gp(lambda q: q.iota(T.key[:, 256:384], [[128, 2], [0, 32], [64, 2]], 0, 0, **flag), [], ["key2"], 128, base=0.13)
-        pe([[T.pa[:, 0:384], T.key[0:1, 0:128], T.ones[0:1, 0:384], True, True]], ["key0", "ones"], ["pa"])
-        vec(lambda q: q.tensor_tensor(T.tri[:], T.pa[:, 0:384], T.key[:], ALU.is_lt), ["key0", "key1", "key2"], ["pa", "tri"], 384)
+
+    def constants():
+        vec(lambda q: q.tensor_scalar(T.xl[:], T.xs[:], 0.0, float(OFFS), ALU.is_ge, ALU.mult), ["xs"], ["xl"], S // 2)
+        for k, v in enumerate([0.125, 65536.0, -65536.0, -0.125]):
+            vec(lambda q, k=k, v=v: q.memset(T.eig[:, k * 64:k * 64 + 64], v), [], ["eig%d" % k], 64)
+        vec(lambda q: q.memset(T.cst[0:1, :], -7.0 / 16), [], ["cst"], 64)
+        vec(lambda q: q.memset(T.scn[:], 0.0), [], ["scn%d" % s for s in range(NS)], NS * 136)
+        gp(lambda q: q.iota(T.pidx[:, 0:1], [[0, 1]], 0, 1), [], ["pidx"], 2, base=0.13)
+        for k, (pattern, base) in enumerate([([[1, 128]], 0), ([[32, 4], [0, 32]], 32), ([[32, 4], [0, 32]], 0)]):
+            gp(lambda q, k=k, pattern=pattern, base=base: q.affine_select(T.tri[:, k * 128:k * 128 + 128], T.ones[:], pattern, ALU.is_gt, 0.0, base, -1),
+               ["ones"], ["tri%d" % k], 128)
         gp(lambda q: q.iota(T.elc[:, 0:8], [[8, 8]], 7 - 128, 0, **flag), [], ["elc"], 8, base=0.13)
-        gp(lambda q: q.iota(T.lqc[:], [[1, 240]], -112, 0, **flag), [], ["lqc"], 240, base=0.13)
         gp(lambda q: q.iota(T.negr[:], [[0, 8], [-1, 8]], 0, 0, **flag), [], ["negr"], 64, base=0.13)
         vec(lambda q: q.tensor_scalar(T.negr[:], T.negr[:], 0.125, None, ALU.mult), ["negr"], ["negr"], 64)
-        gp(lambda q: q.affine_select(T.zsel[:], T.eig[:], [[0, 2], [-16, 8], [0, 8]], ALU.is_ge, 0.0, 0, 1), ["eig0", "eig1"], ["zsel"], 128)
-        gp(lambda q: q.affine_select(T.zsel[:], T.zsel[:], [[0, 2], [16, 8], [0, 8]], ALU.is_ge, 0.0, 15, -1), ["zsel"], ["zsel"], 128)
-        gp(lambda q: q.affine_select(T.tri[:, 0:128], T.tri[:, 0:128], [[1, 128]], ALU.not_equal, -8192.0, 0, -1), ["tri"], ["tri"], 128)
+        gp(lambda q: q.affine_select(T.zsel[:], T.eig[:], [[0, 4], [-16, 8], [0, 8]], ALU.is_ge, 0.0, 0, 1), ["eig%d" % k for k in range(4)], ["zsel0", "zsel1"], 256)
         gp(lambda q: q.iota(T.creg[:], [[0, 16], [4, 8]], 48, 0, **flag), [], ["creg"], 128, base=0.13)
+        gp(lambda q: q.affine_select(T.zsel[:, 64:192], T.zsel[:, 64:192], [[0, 2], [16, 8], [0, 8]], ALU.is_ge, 0.0, 0, -1), ["zsel1"], ["zsel1"], 128)
+        for k in (0, 3):
+            gp(lambda q, k=k: q.affine_select(T.zsel[:, k * 64:k * 64 + 64], T.zsel[:, k * 64:k * 64 + 64], [[16, 8], [0, 8]], ALU.is_ge, 0.0, 15, -1),
+               ["zsel0"], ["zsel0"], 64)
         gp(lambda q: q.iota(T.dmp[:], [[256, 4], [0, 32]], 2048, 2, **flag), [], ["dmp"], 128, base=0.13)
+        gp(lambda q: q.iota(T.lqc[:], [[1, 240]], -112, 0, **flag), [], ["lqc"], 240, base=0.13)
         gp(lambda q: q.affine_select(T.dmp[:], T.dmp[:], [[0, 16], [1, 8]], ALU.is_equal, -10000.0, 0, 0), ["dmp"], ["dmp"], 128)
+        gp(lambda q: q.affine_select(T.tri[:, 0:128], T.tri[:, 0:128], [[1, 128]], ALU.not_equal, -8192.0, 0, -1), ["tri0"], ["tri0"], 128)
         for k, (op, v) in enumerate([(ALU.bitwise_and, 7), (ALU.bitwise_and, 8), (ALU.bitwise_and, 15), (ALU.arith_shift_right, 4)]):
             vec(lambda q, k=k, op=op, v=v: q.tensor_scalar(T.pq[:, k:k + 1], T.pidx[:, 0:1], v, None, op), ["pidx"], ["pq%d" % k], 1)
         vec(lambda q: q.tensor_tensor(T.pf[:, 0:1], T.pq[:, 0:1], T.pq[:, 3:4], ALU.is_equal), ["pq0", "pq3"], ["pf0"], 1)
@@ -120,123 +138,129 @@ def build(T, rank, core, topo, P):
         vec(lambda q: q.tensor_scalar(T.lq[:], T.lqc[:], T.pf[:, 2:3], None, ALU.is_equal), ["lqc", "pf2"], ["lq"], 240)
         vec(lambda q: q.tensor_scalar(T.els[:], T.elc[:, 8:16], 128.0, None, ALU.add), ["eld"], ["els"], 8)
 
-    cnt = {"pn": 0, "ph": 0, "pw": 0}
-
-    def bank(k):
-        cnt[k] += 1
-        return "%s%d" % (k, cnt[k] % 2)
-
-    def came(s, t, a, lo=0, hi=CAP):
-        if t < 0: return T.xs[s * W:(s + 1) * W, a * CAP + lo:a * CAP + hi]
+    def came(s, t, a, lo=0, hi=CAP, step=1):
+        if t < 0: return T["xs" if t == -1 else "xl"][s * W:(s + 1) * W, a * CAP + lo:a * CAP + hi:step]
         if a == rank:
             o = (s * RO + t) * SW + rank * 512
-            return T.snd[:, o + lo:o + hi]
+            return T.snd[:, o + lo:o + hi:step]
         o = (s * RO + t) * S + a * CAP
-        return T.lnd[:, o + lo:o + hi]
+        return T.lnd[:, o + lo:o + hi:step]
 
     def ply(s, t):
         c0, t0 = s * C, s * 128
         k0, k1 = (0, 128) if t else (s * W, (s + 1) * W)
         w0 = (s * RO + t) * SW
-        for r in range(N):
-            gp(lambda q, a=w0 + r * 512: q.iota(T.snd[:, a:a + CAP], [[0, CAP]], 0, 0, **flag), [], ["sz%d.%d.%d" % (s, t, r)], CAP, base=0.13)
-        col = lambda u: ((rank // 2) ^ u) * 64
+        steps = P["steps"][t * NS + s].split()
+        pair = lambda u: u ^ (rank // 2)
+        col = lambda u: pair(u) * 64
         span = lambda us: (min(col(u) for u in us), max(col(u) for u in us) + 64)
-        pw = [bank("pw"), bank("pw")]
         ph = {}
-        for step in P["steps"].split():
+        for step in steps:
             if step[0] == "f": ph.update(dict.fromkeys([int(x) for x in step[1:]], bank("ph")))
 
         def sources(u):
             R, ext = (["snd%d.%d" % (s, t - 1)], (s, t - 1, u)) if t else (["xs"], None)
-            return R, ext, [(i, e, came(s, t - 1, col(u) // 32 + e, 32 * i, 32 * i + 32)) for i in range(2) for e in range(2)]
+            return R, ext, [(i, e, 2 * pair(u) + e) for e in (rank % 2, 1 - rank % 2) for i in range(2)]
+
+        def offsets(pn, u, lo, n, names):
+            o = c0 + col(u) + lo
+            vec(lambda q: q.tensor_scalar(T.off[:, o:o + n], T[pn][:, lo:lo + n], 16 - 273.0 * OFFS if t else 16.0, 0.0, ALU.add, ALU.max), [], [pn] + names, n)
 
         def numbers(u):
             R, ext, four = sources(u)
-            pn = bank("pn")
-            for half in range(2):
-                z = qb(s, half) + 8 * half
-                pe([[T[pn][:, half * 32:half * 32 + 32], T.zq[k0:k1, z - W * i - 8 * e:z - W * i - 8 * e + 128], src, k == 0, k == 3]
-                    for k, (i, e, src) in enumerate(four)], R + ["zq%d.%d.%d" % (s, half, i) for i in (range(2) if t else [s])], [pn], ext=ext)
-            o = c0 + col(u)
-            vec(lambda q: q.tensor_scalar(T.off[:, o:o + 64], T[pn][:, 0:64], 16 - 273.0 * OFFS, 0.0, ALU.add, ALU.max), [], [pn, "off%d.%d" % (s, u)], 64)
+            pn, z, nm = bank("pn"), qb(s, 2), ["off%d.%d.%d" % (s, u, half) for half in range(2)]
+            if u == 3:
+                pe([[T[pn][:, half * 32 + e * 16:half * 32 + e * 16 + 16], T.zq[k0:k1, qb(s, half) + 8 * (half - d) - W * i:qb(s, half) + 8 * (half - d) - W * i + 128],
+                     came(s, t - 1, a, 32 * i + d, 32 * i + 32, 2), half + k + d == 0, half + k + d == 5]
+                    for half in range(2) for k, (i, e, a) in enumerate(four) for d in range(2)], R + ["zq%d.0" % s, "zq%d.1" % s], [pn], ext=ext)
+                return offsets(pn, u, 0, 64, nm)
+            for k in range(2):
+                if k and u == 0 and t: pn = bank("pn")
+                pe([[T[pn][:, e * 32:e * 32 + 32], T.zq[k0:k1, z - W * i:z - W * i + 128], came(s, t - 1, a, 32 * i, 32 * i + 32), i == 0, i == 1]
+                    for i, e, a in four[2 * k:2 * k + 2]], R + ["zq%d.2" % s], [pn], ext=ext if k or u else None)
+                if u == 0 and t: offsets(pn, u, four[2 * k][1] * 32, 32, [nm[four[2 * k][1]]])
+            if u or not t: offsets(pn, u, 0, 64, nm)
 
         def sums(u):
             R, ext, four = sources(u)
-            o = col(u) % 128
+            o, pw, apart = col(u) % 128, "pw%d" % (u // 2), u == 3 or u == 0 and t
             names = [["gat%d.%d.%d.%d" % (s, u, half, k) for k in range(32 // UC)] for half in range(2)]
-            for half in range(2):
+            for half in (rank % 2, 1 - rank % 2) if u == 0 and t else (0, 1):
                 for k in range(32 // UC):
-                    add("VS", None, ["off%d.%d" % (s, u), "tabz%d" % s, "tab%d.0" % s, "tab%d.1" % s], [names[half][k]],
-                        UC * 16 * P["c"] * cyc, gat=(s, t, u, half * (u in P["split"])), col=c0 + col(u) + half * 32 + k * UC)
-            pe([[T[pw[u // 2]][:, o + e:o + 64:2], T.zf[k0:k1, W - W * i:W - W * i + 128], src, k == 0 and u % 2 == 0, False]
-                for k, (i, e, src) in enumerate(four)], R + ["zf0", "zf1"], [pw[u // 2]], ext=ext)
+                    add("VS", None, ["off%d.%d.%d" % (s, u, half), "tabz%d" % s] + ["tab%d.%d.%d" % (s, i, j) for i in range(2) for j in range(8)],
+                        [names[half][k]], UC * 16 * P["c"] * cyc, gat=(s, t, u, half if apart else 0), col=c0 + col(u) + half * 32 + k * UC)
+            pe([[T[pw][:, o + e * 32:o + e * 32 + 32], T.zf[k0:k1, W - W * i:W - W * i + 128], came(s, tt, a, 32 * i, 32 * i + 32),
+                 tt == t - 1 and k == 0 and u % 2 == 0, False] for tt in ([t - 1] if t else [-1, -2]) for k, (i, e, a) in enumerate(four)],
+               R + ["zf0", "zf1"] + ["xl"] * (t == 0), [pw], ext=ext)
+            g0 = (c0 + col(u)) * 16
             for half in range(2):
-                g0 = (c0 + col(u) + half * 32) * 16
-                pe([[T[ph[u]][:, o:o + 64], T.idn[:], T.gat[:, g0 + j:g0 + 512:8], j == 0 and half == 0, j == 7 and half == 1]
-                    for j in range(8)], ["idn"] + (names[half] if u in P["split"] else names[0] + names[1]), [ph[u]])
+                pe([[T[ph[u]][:, o:o + 64], T.idn[:], T.gat[:, g0 + half * 512 + j:g0 + half * 512 + 512:8] if u == 3 else T.gat[:, g0 + half * 8 + j:g0 + 1024:16],
+                     j == 0 and half == 0, j == 7 and half == 1] for j in range(8)], ["idn"] + (names[half] if u == 3 else names[0] + names[1]), [ph[u]])
 
         def fire(us):
             lo, hi = span(us)
-            b, o, n = ph[us[0]], lo % 128, hi - lo
-            if P["rel"] == "V":
-                vec(lambda q: q.tensor_scalar(T.rel[:, c0 + lo:c0 + hi], T[b][:, o:o + n], 0.0, 2.0 ** -8, ALU.max, ALU.mult), [], [b, "rel%d.%d" % (s, us[0])], n)
-            else:
-                vec(lambda q: q.activation(T.rel[:, c0 + lo:c0 + hi], T[b][:, o:o + n], ACT.Relu, scale=2.0 ** -8), [], [b, "rel%d.%d" % (s, us[0])], n, eng="S")
-            pe([[T[pw[us[0] // 2]][:, o:o + n], T.polh[:, t0:t0 + 128], T.rel[:, c0 + lo:c0 + hi], False, us[-1] % 2 == 1]],
-               ["polh%d" % s, "rel%d.%d" % (s, us[0])], [pw[us[0] // 2]])
+            b, o, n, pw = ph[us[0]], lo % 128, hi - lo, "pw%d" % (us[0] // 2)
+            vec({"V": lambda q: q.tensor_scalar(T.rel[:, c0 + lo:c0 + hi], T[b][:, o:o + n], 0.0, 2.0 ** -8, ALU.max, ALU.mult),
+                 "S": lambda q: q.activation(T.rel[:, c0 + lo:c0 + hi], T[b][:, o:o + n], ACT.Relu, scale=2.0 ** -8)},
+                [], [b, "rel%d.%d" % (s, us[0])], n, eng=P["rel"])
+            pe([[T[pw][:, o:o + n], T.polh[:, t0:t0 + 128], T.rel[:, c0 + lo:c0 + hi], False, us[-1] % 2 == 1]], ["polh%d" % s, "rel%d.%d" % (s, us[0])], [pw])
 
         def changed(us):
             lo, hi = span(us)
-            b, o = pw[us[0] // 2], lo % 128
-            vec(lambda q: q.tensor_scalar(T.vv[:, c0 + lo:c0 + hi], T[b][:, o:o + hi - lo], HALF, 17.0 / 32, ALU.add, ALU.max),
-                [], [b] + ["vv%d.%d" % (s, u) for u in us], hi - lo)
+            b, o = "pw%d" % (us[0] // 2), lo % 128
+            vec({"V": lambda q: q.tensor_scalar(T.vv[:, c0 + lo:c0 + hi], T[b][:, o:o + hi - lo], HALF, None, ALU.add),
+                 "S": lambda q: q.activation(T.vv[:, c0 + lo:c0 + hi], T[b][:, o:o + hi - lo], ACT.Identity, bias=HALF)},
+                [], [b] + ["vv%d.%d" % (s, u) for u in us], hi - lo, eng=P["vv"])
 
         def route(cr):
             cc = (rank // 4) ^ cr
-            vs, m0, a0 = T.vv[:, c0 + cc * 128:c0 + cc * 128 + 128], t0 + cc * 64, cc * 64
-            out, one = T.pt[:, 0:64], T.ones[0:1, 0:128]
-            pe([[out, one, T.cst[0:1, 0:64], True, False]], ["ones", "cst0"], ["pt"])
-            pe([[out, vs, T.zsel[:, 0:64], False, False], [out, one, T.cst[0:1, 64:128], False, False], [out, one, T.cst[0:1, 128:192], False, False],
-                [out, vs, T.zsel[:, 64:128], False, True]], ["zsel", "cst1", "cst2", "vv%d.%d" % (s, 2 * cr), "vv%d.%d" % (s, 2 * cr + 1)], ["pt"], step=4)
+            vs, m0, a0, out = T.vv[:, c0 + cc * 128:c0 + cc * 128 + 128], t0 + cc * 64, cc * 64, T.pt[:, 0:64]
+            pe([[out, T.ones[0:1, 0:128], T.cst[0:1, :], True, False]], ["ones", "cst"], ["pt"])
+            pe([[out, vs, T.zsel[:, k * 64:k * 64 + 64], False, k == 3] for k in range(4)],
+               ["zsel0", "zsel1", "vv%d.%d" % (s, 2 * cr), "vv%d.%d" % (s, 2 * cr + 1)], ["pt"], step=4)
             vec(lambda q: q.tensor_tensor(T.mb[:, m0:m0 + 64], out, T.negr[:], ALU.is_equal), ["negr"], ["pt", "mb%d.%d" % (s, cr)], 64)
             if cr == 0: pe([[T.pa[:, 0:128], T.ones[:, 0:128], T.creg[:], True, False]], ["ones", "creg"], ["pa"])
-            mms = [[T.pa[:, a0 + o:a0 + o + n], T.tri[:, k * 128:k * 128 + 128], T.mb[:, m0 + i:m0 + i + n], False, False]
-                   for k, o, i, n in [(0, 0, 0, 64), (1, 32, 0, 32), (2, 0, 32, 32)]]
-            if cc == 0: mms += [[T.pa[:, o:o + n], T.ones[:, 0:128], T.mb[:, m0 + i:m0 + i + n], False, False] for o, i, n in [(64, 0, 64), (64, 32, 32), (96, 0, 32)]]
+            three = [(0, 0, 64), (32, 0, 32), (0, 32, 32)]
+            mms = [[T.pa[:, a0 + o:a0 + o + n], T.tri[:, k * 128:k * 128 + 128], T.mb[:, m0 + i:m0 + i + n], False, False] for k, (o, i, n) in enumerate(three)]
+            if cc == 0: mms += [[T.pa[:, 64 + o:64 + o + n], T.ones[:, 0:128], T.mb[:, m0 + i:m0 + i + n], False, False] for o, i, n in three]
             mms[-1][4] = cr == 1
-            add("P", lambda q: [q.matmul(*m) for m in mms][-1], ["mb%d.%d" % (s, cr), "tri", "ones"], ["pa"], 384 * P["pe"] * P["f"])
+            add("P", lambda q: [q.matmul(*m) for m in mms][-1], ["mb%d.%d" % (s, cr), "tri0", "tri1", "tri2"], ["pa"], 384 * P["pe"] * P["f"])
 
-        for step in P["steps"].split():
-            us = [int(x) for x in step[1:]]
-            {"n": numbers, "s": sums, "r": route, "f": fire, "c": changed}[step[0]](us if step[0] in "fc" else us[0])
         vvs = ["vv%d.%d" % (s, u) for u in range(4)]
-        z0 = s * 136
-        vec(lambda q: q.tensor_tensor_scan(T.scn[:, z0:z0 + 128], T.dmp[:], T.pa[:, 0:128], -10000.0, ALU.max, ALU.min),
-            ["dmp"], ["pa", "scn%d" % s], 128)
-        vec(lambda q: q.tensor_copy(T.ee[:, t0:t0 + 128], T.scn[:, z0:z0 + 136].indirect(T.els[:])),
-            ["scn%d" % s, "scz%d" % s, "els"], ["ee%d" % s], 60 + 128 * P["c"])
-        pe([[T.pa[:, 0:16], T.lq[:, 112 - 16 * h:240 - 16 * h], T.ee[:, t0 + h * 16:t0 + (h + 1) * 16], h == 0, h == 7] for h in range(8)],
-           ["lq", "ee%d" % s], ["pa"], step=8)
-        vec(lambda q: q.tensor_scalar(T.pos[:, s * 16:(s + 1) * 16], T.pa[:, 0:16], 2048.0, None, ALU.add), [], ["pa", "pos%d" % s], 16)
-        vec(lambda q: q.tensor_scalar(T.wr[:, c0:c0 + C], T.vv[:, c0:c0 + C], OFFS + 16.0, -16.0, ALU.is_ge, ALU.mult), vvs, ["wr%d" % s], 128)
+
+        def places(k):
+            z0 = s * 136
+            vec(lambda q: q.tensor_tensor_scan(T.scn[:, z0:z0 + 128], T.dmp[:], T.pa[:, 0:128], -10000.0, ALU.max, ALU.min), ["dmp"], ["pa", "scn%d" % s], 128)
+            vec(lambda q: q.tensor_copy(T.ee[:, t0:t0 + 128], T.scn[:, z0:z0 + 136].indirect(T.els[:])), ["scn%d" % s, "els"], ["ee%d" % s], 60 + 128 * P["c"])
+            pe([[T.pa[:, 0:16], T.lq[:, 112 - 16 * h:240 - 16 * h], T.ee[:, t0 + h * 16:t0 + (h + 1) * 16], h == 0, h == 7] for h in range(8)],
+               ["lq", "ee%d" % s], ["pa"], step=8)
+            vec(lambda q: q.tensor_scalar(T.pos[:, s * 16:(s + 1) * 16], T.pa[:, 0:16], 2048.0, None, ALU.add), [], ["pa", "pos%d" % s], 16)
+            vec(lambda q: q.tensor_scalar(T.wr[:, c0:c0 + C], T.vv[:, c0:c0 + C], OFFS + 16.0, -16.0, ALU.is_ge, ALU.mult), vvs, ["wr%d" % s], 128)
+
+        for step in steps:
+            us = [int(x) for x in step[1:]]
+            if step == "|": yield
+            elif step == "K": constants()
+            else: {"n": numbers, "s": sums, "r": route, "f": fire, "c": changed, "p": policy, "q": places}[step[0]](us if step[0] in "fc" else us[0])
+        zero = ["sz%d.%d.%d" % (s, t, r) for r in range(N)]
+        for r in range(N):
+            gp(lambda q, a=w0 + r * 512: q.iota(T.snd[:, a:a + CAP], [[0, CAP]], 0, 0, **flag), [], [zero[r]], CAP, base=0.13)
         vec(lambda q: q.tensor_tensor(T.snd[:, w0:w0 + SW].indirect(T.pos[:, s * 16:(s + 1) * 16]), T.vv[:, c0:c0 + C], T.wr[:, c0:c0 + C], ALU.add),
-            vvs + ["wr%d" % s, "pos%d" % s] + ["sz%d.%d.%d" % (s, t, r) for r in range(N)], ["snd%d.%d" % (s, t)], 60 + C * P["sc"])
-        for call in P["last" if t == RO - 1 else "calls"]:
-            def send(q, call=call):
-                trs, e0 = [], 0
-                for rel, ne in call:
-                    dst = T.cores[rank ^ rel]
-                    rid, pid = topo.addr(dst)[0:2]
-                    eng = topo.engines(core, dst)[e0:e0 + ne]
-                    e0 += ne
-                    o = w0 + (rank ^ rel) * 512
-                    lo = (s * RO + t) * S + rank * CAP
+            vvs + ["wr%d" % s, "pos%d" % s] + zero, ["snd%d.%d" % (s, t)], 60 + C * P["sc"])
+        for x in range(4):
+            dsts = [rank ^ rel for rel in (2 * x, 2 * x + 1) if rel]
+
+            def send(q, x=x, dsts=dsts):
+                trs = []
+                for j, r in enumerate(dsts):
+                    rid, pid = topo.addr(T.cores[r])[0:2]
+                    eng = topo.engines(core, T.cores[r])
+                    eng = eng[j * len(eng) // len(dsts):(j + 1) * len(eng) // len(dsts)]
+                    o, lo = w0 + r * 512, (s * RO + t) * S + rank * CAP
                     trs.append(RemoteDMATransfer(dst_ids=[DstId(rid=rid, pnc=pid)], dma_engine_mask=sum(1 << e for e in eng),
-                                                 remote_sem=T.sem["ar%d_%d_%d" % (s, t, rel // 2)],
-                                                 src=T.snd[:, o:o + CAP], dst=T.lnd[:, lo:lo + CAP]))
+                                                 remote_sem=T.sem["ar%d_%d_%d" % (s, t, x)], src=T.snd[:, o:o + CAP], dst=T.lnd[:, lo:lo + CAP]))
                 return q.remote_dma_fused(trs, local_sem=T.sem.sent)
-            add("G", send, ["snd%d.%d" % (s, t)], [], P["call"], call=call, st=(s, t))
+            add("G", send, ["snd%d.%d" % (s, t)], [], P["call"], call=len(dsts), st=(s, t, x))
 
     def last(s):
         for cr in range(2):
@@ -249,28 +273,25 @@ def build(T, rank, core, topo, P):
             o = s * C + cc * 128
             vec(lambda q, pn=pn, o=o: q.tensor_scalar(T.yo[:, o:o + 128], T[pn][:, 0:128], -float(OFFS), -1.0, ALU.add, ALU.max),
                 [], [pn, "yo%d.%d" % (s, cr)], 128)
-            for i in range(2):
-                a = (4 * cc + 2 * i) * CAP
-                dma("YS"[i], T.y[s * W:(s + 1) * W, a:a + 128], T.yo[i * W:(i + 1) * W, o:o + 128], ["yo%d.%d" % (s, cr)], [], W, 256, sem="st")
+            for ss, c in [(0, 0), (0, 1), (1, 0)] * (cr == 0) + [(1, 1)] * cr if s else []:
+                for i in range(2):
+                    a, o = (4 * ((rank // 4) ^ c) + 2 * i) * CAP, ss * C + ((rank // 4) ^ c) * 128
+                    dma("YS"[i], T.y[ss * W:(ss + 1) * W, a:a + 128], T.yo[i * W:(i + 1) * W, o:o + 128], ["yo%d.%d" % (ss, c), "yo1.%d" % cr], [], W, 256, sem="st")
 
-    vec(lambda q: q.memset(T.polb[:], 0.0), [], ["polz"], NS * 64)
-    vec(lambda q: q.memset(T.zq[:], 0.0), [], ["zq%d.%d.%d" % (s, h, i) for s in range(NS) for h in range(2) for i in range(2)], T.zq.shape[1] // 2)
-    gp(lambda q: q.iota(T.msk[:], [[0, 5], [-1, 2], [0, 8]], 1, 0, **flag), [], ["msk"], 80, base=0.13)
+    dma("Y", T.plr[:], T.pl[:], [], ["plr"], 128, 256)
     dma("S", T.xs[:], T.x[:], [], ["xs"], 128, 2 * S)
-    dma("Y", T.plr[:, 0:128], T.pl[:], [], ["plr"], 128, 256)
-    for s in range(NS): loads(s)
     for s in range(NS):
-        dma("Y", T.plr[(1 - s) * W:(2 - s) * W, 128:128 + W], T.pl[s * W:(s + 1) * W, s * W:(s + 1) * W], [], ["plr%d" % s], W, 2 * W)
-    vec(lambda q: q.tensor_scalar(T.xl[:], T.xs[:], 0.0, float(OFFS), ALU.is_ge, ALU.mult), ["xs"], ["xl"], S // 2)
-    vec(lambda q: q.tensor_tensor(T.xs[:], T.xs[:], T.xl[:], ALU.add), ["xl"], ["xs"], 2 * S)
-    for s in range(NS): halves(s, s)
-    own_constants(0)
-    constants()
-    for t in range(RO):
-        for s in range(NS):
-            if s and not t: own_constants(s)
-            if t == 1: halves(s, 1 - s)
-            ply(s, t)
+        tables(s)
+        if s == P["polat"]: dma("Y", T.polr[:], T.pol[:], [], ["polr"], 128, 256)
+    first_constants()
+    copies()
+    for s in range(NS): placements(s)
+    plies = [ply(s, t) for t in range(RO) for s in range(NS)]
+    next(plies[0])
+    for k, p in enumerate(plies):
+        next(p)
+        if k + 1 < len(plies): next(plies[k + 1])
+        next(p, None)
     for s in range(NS): last(s)
     return ops
 
@@ -299,19 +320,20 @@ def joins(p, o):
     return "gat" in p and p["gat"] == o["gat"] and abs(p["col"] - o["col"]) == UC
 
 
-def place(ops, P, order=None):
+def place(ops, P, order=None, seq=None):
     fin, arr, start, on = {}, {}, {}, {}
     busy = {e: [] for e in "VSPGY"}
-    eng, first, pool = [0.0] * 16, P["first"], {}
+    eng, first, pool = 0.0, P["first"], {}
     for o in ops:
         if "gat" in o: pool.setdefault(o["gat"], []).append(o)
-    for i, es in order or [(o["i"], o["eng"]) for o in ops]:
+    for i, es in order or [(o["i"], o["eng"]) for o in seq or ops]:
         best = None
         for e in es:
-            o = ops[i] if len(es) == 1 else pool[ops[i]["gat"]][0 if e == "S" else -1]
+            o = pool[ops[i]["gat"]][0 if e == "S" else -1] if "gat" in ops[i] and not order else ops[i]
             d, t = o["dur"], 0.0
             for k in o["deps"]:
                 t = max(t, fin[k] + (0.0 if on[k] == e == "P" else P["wake"] if "sem" in ops[k] else P["lat"]))
+            if not order and e == "V" and "gat" not in o: t += P["pad"].get(o["W"][-1].split(".")[0], 0.0)
             if o.get("ext"): t = max(t, arr[o["ext"]] + P["wake"])
             if o.get("after") is not None: t = max(t, start[o["after"]] + 1e-3)
             b = busy[e]
@@ -320,31 +342,22 @@ def place(ops, P, order=None):
             while True:
                 if k: t = max(t, b[k - 1][1])
                 new = "gat" in o and not (k and t == b[k - 1][1] and joins(ops[b[k - 1][2]], o))
-                if k == len(b) or t + d + 0.06 * new + P["room"] * ("gat" in o) <= b[k][0]: break
+                if k == len(b) or t + d + 0.06 * new <= b[k][0]: break
                 k += 1
             x = t + d + 0.06 * new
-            cost = x + P["join"] * new + P["lean"] * (e == "V")
+            cost = x + (P["join"] * new if "gat" in o else P["lean"] * (e == "V"))
             if best is None or cost < best[0]: best = (cost, e, k, t, x, o)
         _, e, k, t, x, o = best
         i = o["i"]
-        if len(es) > 1: pool[o["gat"]].remove(o)
+        if "gat" in o: pool[o["gat"]].remove(o)
         busy[e].insert(k, (t, x, i))
         start[i], fin[i], on[i] = t, x, e
         if "sem" in o:
-            fin[i] = max([t + P["dma0"]] + eng * (o["sem"] != "st")) + o["rows"] / 16 * (P["row"] + o["nb"] / P["bw"])
-            if o["sem"] != "st": eng = [fin[i]] * 16
+            eng = fin[i] = max(t + P["dma0"], eng) + o["rows"] / 16 * (P["row"] + o["nb"] / P["bw"])
         if "call" in o:
-            t0, e0, first = x + P["dma0"] + first, 0, 0.0
-            for rel, ne in o["call"]:
-                x = max([t0] + eng[e0:e0 + ne]) + 128 / ne * (P["row"] + 128 / P["bw"])
-                eng[e0:e0 + ne] = [x] * ne
-                e0 += ne
-                key = o["st"] + (rel // 2,)
-                arr[key] = max(arr.get(key, 0.0), x)
+            eng = arr[o["st"]] = max(x + P["dma0"] + first, eng) + 8 * o["call"] * (P["row"] + 128 / P["bw"])
+            first = 0.0
     return [(i, on[i]) for i in sorted(start, key=lambda i: (start[i], i))], max(fin.values()), busy
-
-
-PLAN = {}
 
 
 def rank_program(g, core, T, topo):
@@ -353,10 +366,9 @@ def rank_program(g, core, T, topo):
         return
     ops = build(T, rank, core, topo, PAR)
     depend(ops)
-    if "order" not in PLAN: PLAN["order"] = place(ops, PAR)[0]
     queues = {"V": g.vector, "S": g.scalar, "P": g.tensor, "G": g, "Y": g.sync}
     items, item_of, lastq = [], {}, {}
-    for i, e in PLAN["order"]:
+    for i, e in place(ops, PAR)[0]:
         o, p = ops[i], lastq.get(e)
         if "gat" in o and p is not None and joins(p["ops"][-1], o) and all(d in p["deps"] or d in p["seen"] for d in o["deps"]):
             p["ops"].append(o)
@@ -384,17 +396,13 @@ def rank_program(g, core, T, topo):
         p["waits"] = waits
         p["clock"] = dict(kn)
     count = {e: 0 for e in queues}
-    sent, stores = 0, 0
+    sent, stores, engines = 0, 0, len(topo.engines(core, T.cores[rank ^ 1]))
     for p in items:
         e, q, o = p["e"], queues[p["e"]], p["ops"][0]
         for w in p["waits"]:
-            if "ext" in w:
-                s, t, u = w["ext"]
-                q.wait_ge(T.sem["ar%d_%d_%d" % (s, t, u)], sum(ne for call in PAR["last" if t == RO - 1 else "calls"] for rel, ne in call if rel // 2 == u))
-            elif "sem" in w["ops"][0]:
-                q.wait_ge(T.sem[w["ops"][0]["sem"]], 16)
-            else:
-                q.wait_ge(T.sem["e" + w["e"]], w["n"])
+            if "ext" in w: q.wait_ge(T.sem["ar%d_%d_%d" % w["ext"]], engines)
+            elif "sem" in w["ops"][0]: q.wait_ge(T.sem[w["ops"][0]["sem"]], 16)
+            else: q.wait_ge(T.sem["e" + w["e"]], w["n"])
         if "gat" in o:
             s = o["gat"][0]
             lo = min(x["col"] for x in p["ops"])
@@ -403,12 +411,12 @@ def rank_program(g, core, T, topo):
             out = T.gat[:, lo * 16:hi * 16]
             ins = q.tensor_copy(out, win) if e == "V" else q.activation(out, win, ACT.Copy)
         else:
-            ins = o["fn"](q)
+            ins = (o["fn"][e] if isinstance(o["fn"], dict) else o["fn"])(q)
         if "sem" in o:
             ins.then_inc(T.sem[o["sem"]], 16)
             stores += 16 * (o["sem"] == "st")
         elif "call" in o:
-            sent += sum(ne for rel, ne in o["call"])
+            sent += engines
         elif p["inc"]:
             count[e] += 1
             p["n"] = count[e]

from concourse.bass import DstId, RemoteDMATransfer
from concourse.mybir import AluOpType as ALU, ActivationFunctionType as ACT

N, S, CAP, RO, LW = 8, 512, 64, 3, 4096
NS = 2
W = 64
C = 256
SW = 5120
TB = LW + 16
GAP = 72
OFFS = 132
HALF = 0.5 - 2.0 ** -16
UC = 4
PAR = {"c": 1.56, "sc": 3.8, "f": 1.0, "pe": 0.00042, "lat": 0.2, "join": 0.0, "mm": 1,
       "row": 0.03, "bw": 20000.0, "dma0": 1.0, "call": 0.3, "first": 1.0, "wake": 0.15, "rel": "V", "vv": "VS", "lean": 0.0,
       "polat": 0, "pad": {}, "cuts": [(0, 0, 2), (0, 2, 4), (0, 4, 8), (1, 4, 8)],
       "steps": ["n1 n0 K | n3 s0 n2 p0 s1 s2 f01 c01 s3 f2 f3 r0 c23 r1 | q0", "n2 n0 n1 s0 n3 | s1 | p1 s2 f01 s3 c01 r0 f2 f3 c23 r1 q0",
                 "| n0 n1 s0 n2 s1 s2 n3 f01 s3 c01 f2 r0 f3 c23 r1 q0 |", "n0 n1 n2 s0 n3 s1 s2 f01 s3 | f2 f3 c01 | c23 r0 r1 q0",
                 "n0 n1 | n2 s0 n3 s1 s2 f01 c01 s3 r0 f2 f3 c23 r1 | q0", "n0 n1 s0 n3 s1 n2 f01 s2 s3 c01 | | f2 f3 r0 c23 r1 q0"]}

BF, F32, F16 = "bfloat16", "float32", "float16"
SCRATCH = {k: ("sbuf", [128, n], d) for k, n, d in [
    ("xs", S, BF), ("xl", S, BF), ("tab", NS * TB, BF), ("gat", NS * C * 16, BF), ("snd", NS * RO * SW, BF), ("lnd", NS * RO * S, BF),
    ("plr", 128, BF), ("zq", GAP + 3 * NS * (W + GAP), BF), ("polr", 128, BF), ("polh", NS * 128, F16),
    ("msk", 80, BF), ("ones", 128, BF), ("eig", 256, BF), ("idn", 128, BF), ("zf", 3 * W, BF), ("zsel", 256, BF), ("cst", 64, BF),
    ("negr", 64, BF), ("tri", 384, BF), ("creg", 128, BF), ("dmp", 128, F32), ("pidx", 8, "int32"),
    ("pq", 8, "int32"), ("pf", 8, F32), ("elc", 16, F32), ("els", 8, "uint16"), ("lqc", 240, F32), ("lq", 240, F16),
    ("off", NS * C, "uint16"), ("rel", NS * C, F16), ("vv", NS * C, BF), ("wr", NS * C, BF),
    ("mb", NS * 128, BF), ("scn", NS * 136, F32), ("ee", NS * 128, F16), ("pos", NS * 16, "uint16"), ("yo", NS * C, BF)]}
for _b in ("pn0", "pn1", "ph0", "ph1", "pw0", "pw1", "pt", "pa"):
    SCRATCH[_b] = ("psum", [128, 512], F32)

SEMAPHORES = ["eV", "eS", "eP", "eG", "sent", "st"]
SEMAPHORES += ["ar%d_%d_%d" % (s, t, b) for s in range(NS) for t in range(RO) for b in range(4)]
SEMAPHORES += ["d%d" % i for i in range(12)]


def build(T, rank, core, topo, P):
    ops = []
    cyc = 0.00083 * P["f"]
    ndma = [0]

    def add(eng, fn, R, Wr, dur, **kw):
        o = {"eng": eng, "fn": fn, "R": R, "W": Wr, "dur": dur, "i": len(ops)}
        o.update(kw)
        ops.append(o)

    def vec(fn, R, Wr, n, eng="V", **kw):
        add(eng, fn, R, Wr, max(64, n) * cyc, **kw)

    def gp(fn, R, Wr, n, base=0.17, **kw):
        add("G", fn, R, Wr, base + 2 * n * cyc, **kw)

    def pe(mms, R, Wr, step=None, **kw):
        step = step or P["mm"]
        for k in range(0, len(mms), step):
            add("P", lambda q, part=mms[k:k + step]: [q.matmul(*m) for m in part][-1], R, Wr,
                sum(max(64, m[2].shape[-1]) for m in mms[k:k + step]) * P["pe"] * P["f"], **kw)

    def dma(eng, out, in_, R, Wr, rows, nbytes, **kw):
        if "sem" not in kw:
            ndma[0] += 1
            kw["sem"] = "d%d" % (ndma[0] - 1)
        add(eng, lambda q: q.dma_start(out, in_), R, Wr, 0.06, rows=rows, nb=nbytes, **kw)

    flag = {"allow_small_or_imprecise_dtypes": True}
    qb = lambda s, half: GAP + (3 * s + half) * (W + GAP)
    cnt = {"pn": 0, "ph": 0}

    def bank(k):
        cnt[k] += 1
        return "%s%d" % (k, cnt[k] % 2)

    def tables(s):
        for i, lo, hi in P["cuts"] if s == 0 else [(0, 0, 8), (1, 0, 8)]:
            dma("Y", T.tab[i * W:(i + 1) * W, s * TB + 16 + lo * 512:s * TB + 16 + hi * 512], T.lut[s * W:(s + 1) * W, lo * 512:hi * 512], [],
                ["tab%d.%d.%d" % (s, i, k) for k in range(lo, hi)], W, 1024 * (hi - lo))

    def copies():
        for k in range(min([lo for i, lo, hi in P["cuts"] if i] + [8])):
            b, o = ["pw0", "pw1", "pt", "pa"][k % 4], 16 + k * 512
            pe([[T[b][W:128, :], T.idn[0:W, 0:W], T.tab[0:W, o:o + 512], True, True]], ["idn", "tab0.0.%d" % k], [b])
            if k % 2: vec(lambda q, b=b, o=o: q.tensor_copy(T.tab[W:128, o:o + 512], T[b][W:128, :]), [], [b, "tab0.1.%d" % k], 512)
            else: vec(lambda q, b=b, o=o: q.activation(T.tab[W:128, o:o + 512], T[b][W:128, :], ACT.Copy), [], [b, "tab0.1.%d" % k], 512, eng="S")

    def placements(s):
        p, b = slice(s * W, (s + 1) * W), bank("ph")
        pe([[T[b][:, 0:W], T.zf[p, W - W * i:W - W * i + 128], T.plr[p, p], i == 0, i == 1] for i in range(2)], ["plr", "zf0", "zf1"], [b])
        vec(lambda q: q.tensor_copy(T.zq[:, qb(s, 2):qb(s, 2) + W], T[b][:, 0:W]), [], [b, "zq%d.2" % s], W)
        for half in range(2):
            vec(lambda q, half=half: q.tensor_tensor(T.zq[:, qb(s, half):qb(s, half) + W], T[b][:, 0:W], T.msk[:, 8 * half:8 * half + W], ALU.mult),
                ["msk"], [b, "zq%d.%d" % (s, half)], W)
        vec(lambda q: q.memset(T.tab[:, s * TB:s * TB + 16], 0.0), [], ["tabz%d" % s], 8)

    def policy(s):
        p, b = slice(s * W, (s + 1) * W), bank("pn")
        pe([[T[b][:, i * W:(i + 1) * W], T.zf[p, W - W * i:W - W * i + 128], T.polr[p, p], True, True] for i in range(2)], ["polr", "zf0", "zf1"], [b])
        vec(lambda q: q.tensor_scalar(T.polh[:, s * 128:(s + 1) * 128], T[b][:, 0:128], 2.0 ** -7, None, ALU.mult), [], [b, "polh%d" % s], 128)

    def first_constants():
        vec(lambda q: q.memset(T.ones[:], 1.0), [], ["ones"], 64)
        gp(lambda q: q.affine_select(T.idn[:], T.ones[:, 0:128], [[-1, 128]], ALU.is_equal, 0.0, 0, 1), ["ones"], ["idn"], 128)
        gp(lambda q: q.iota(T.msk[:], [[0, 5], [-1, 2], [0, 8]], 1, 0, **flag), [], ["msk"], 80, base=0.13)
        vec(lambda q: q.memset(T.zf[:], 0.0), [], ["zf0", "zf1"], 96)
        vec(lambda q: q.memset(T.zq[:], 0.0), [], ["zq%d.%d" % (s, h) for s in range(NS) for h in range(3)], T.zq.shape[1] // 2)
        for i in range(2):
            vec(lambda q, i=i: q.tensor_copy(T.zf[i * W:(i + 1) * W, W:2 * W], T.idn[i * W:(i + 1) * W, i * W:(i + 1) * W]), ["idn"], ["zf%d" % i], 32)

    def constants():
        vec(lambda q: q.tensor_scalar(T.xl[:], T.xs[:], 0.0, float(OFFS), ALU.is_ge, ALU.mult), ["xs"], ["xl"], S // 2)
        for k, v in enumerate([0.125, 65536.0, -65536.0, -0.125]):
            vec(lambda q, k=k, v=v: q.memset(T.eig[:, k * 64:k * 64 + 64], v), [], ["eig%d" % k], 64)
        vec(lambda q: q.memset(T.cst[0:1, :], -7.0 / 16), [], ["cst"], 64)
        vec(lambda q: q.memset(T.scn[:], 0.0), [], ["scn%d" % s for s in range(NS)], NS * 136)
        gp(lambda q: q.iota(T.pidx[:, 0:1], [[0, 1]], 0, 1), [], ["pidx"], 2, base=0.13)
        for k, (pattern, base) in enumerate([([[1, 128]], 0), ([[32, 4], [0, 32]], 32), ([[32, 4], [0, 32]], 0)]):
            gp(lambda q, k=k, pattern=pattern, base=base: q.affine_select(T.tri[:, k * 128:k * 128 + 128], T.ones[:], pattern, ALU.is_gt, 0.0, base, -1),
               ["ones"], ["tri%d" % k], 128)
        gp(lambda q: q.iota(T.elc[:, 0:8], [[8, 8]], 7 - 128, 0, **flag), [], ["elc"], 8, base=0.13)
        gp(lambda q: q.iota(T.negr[:], [[0, 8], [-1, 8]], 0, 0, **flag), [], ["negr"], 64, base=0.13)
        vec(lambda q: q.tensor_scalar(T.negr[:], T.negr[:], 0.125, None, ALU.mult), ["negr"], ["negr"], 64)
        gp(lambda q: q.affine_select(T.zsel[:], T.eig[:], [[0, 4], [-16, 8], [0, 8]], ALU.is_ge, 0.0, 0, 1), ["eig%d" % k for k in range(4)], ["zsel0", "zsel1"], 256)
        gp(lambda q: q.iota(T.creg[:], [[0, 16], [4, 8]], 48, 0, **flag), [], ["creg"], 128, base=0.13)
        gp(lambda q: q.affine_select(T.zsel[:, 64:192], T.zsel[:, 64:192], [[0, 2], [16, 8], [0, 8]], ALU.is_ge, 0.0, 0, -1), ["zsel1"], ["zsel1"], 128)
        for k in (0, 3):
            gp(lambda q, k=k: q.affine_select(T.zsel[:, k * 64:k * 64 + 64], T.zsel[:, k * 64:k * 64 + 64], [[16, 8], [0, 8]], ALU.is_ge, 0.0, 15, -1),
               ["zsel0"], ["zsel0"], 64)
        gp(lambda q: q.iota(T.dmp[:], [[256, 4], [0, 32]], 2048, 2, **flag), [], ["dmp"], 128, base=0.13)
        gp(lambda q: q.iota(T.lqc[:], [[1, 240]], -112, 0, **flag), [], ["lqc"], 240, base=0.13)
        gp(lambda q: q.affine_select(T.dmp[:], T.dmp[:], [[0, 16], [1, 8]], ALU.is_equal, -10000.0, 0, 0), ["dmp"], ["dmp"], 128)
        gp(lambda q: q.affine_select(T.tri[:, 0:128], T.tri[:, 0:128], [[1, 128]], ALU.not_equal, -8192.0, 0, -1), ["tri0"], ["tri0"], 128)
        for k, (op, v) in enumerate([(ALU.bitwise_and, 7), (ALU.bitwise_and, 8), (ALU.bitwise_and, 15), (ALU.arith_shift_right, 4)]):
            vec(lambda q, k=k, op=op, v=v: q.tensor_scalar(T.pq[:, k:k + 1], T.pidx[:, 0:1], v, None, op), ["pidx"], ["pq%d" % k], 1)
        vec(lambda q: q.tensor_tensor(T.pf[:, 0:1], T.pq[:, 0:1], T.pq[:, 3:4], ALU.is_equal), ["pq0", "pq3"], ["pf0"], 1)
        vec(lambda q: q.tensor_scalar(T.pf[:, 1:2], T.pq[:, 1:2], 8.0, None, ALU.mult), ["pq1"], ["pf1"], 1)
        vec(lambda q: q.tensor_copy(T.pf[:, 2:3], T.pq[:, 2:3]), ["pq2"], ["pf2"], 1)
        vec(lambda q: q.tensor_scalar(T.elc[:, 8:16], T.elc[:, 0:8], T.pf[:, 1:2], T.pf[:, 0:1], ALU.add, ALU.mult), ["elc", "pf0", "pf1"], ["eld"], 8)
        vec(lambda q: q.tensor_scalar(T.lq[:], T.lqc[:], T.pf[:, 2:3], None, ALU.is_equal), ["lqc", "pf2"], ["lq"], 240)
        vec(lambda q: q.tensor_scalar(T.els[:], T.elc[:, 8:16], 128.0, None, ALU.add), ["eld"], ["els"], 8)

    def came(s, t, a, lo=0, hi=CAP, step=1):
        if t < 0: return T["xs" if t == -1 else "xl"][s * W:(s + 1) * W, a * CAP + lo:a * CAP + hi:step]
        if a == rank:
            o = (s * RO + t) * SW + rank * 512
            return T.snd[:, o + lo:o + hi:step]
        o = (s * RO + t) * S + a * CAP
        return T.lnd[:, o + lo:o + hi:step]

    def ply(s, t):
        c0, t0 = s * C, s * 128
        k0, k1 = (0, 128) if t else (s * W, (s + 1) * W)
        w0 = (s * RO + t) * SW
        steps = P["steps"][t * NS + s].split()
        pair = lambda u: u ^ (rank // 2)
        col = lambda u: pair(u) * 64
        span = lambda us: (min(col(u) for u in us), max(col(u) for u in us) + 64)
        ph = {}
        for step in steps:
            if step[0] == "f": ph.update(dict.fromkeys([int(x) for x in step[1:]], bank("ph")))

        def sources(u):
            R, ext = (["snd%d.%d" % (s, t - 1)], (s, t - 1, u)) if t else (["xs"], None)
            return R, ext, [(i, e, 2 * pair(u) + e) for e in (rank % 2, 1 - rank % 2) for i in range(2)]

        def offsets(pn, u, lo, n, names):
            o = c0 + col(u) + lo
            vec(lambda q: q.tensor_scalar(T.off[:, o:o + n], T[pn][:, lo:lo + n], 16 - 273.0 * OFFS if t else 16.0, 0.0, ALU.add, ALU.max), [], [pn] + names, n)

        def numbers(u):
            R, ext, four = sources(u)
            pn, z, nm = bank("pn"), qb(s, 2), ["off%d.%d.%d" % (s, u, half) for half in range(2)]
            if u == 3:
                pe([[T[pn][:, half * 32 + e * 16:half * 32 + e * 16 + 16], T.zq[k0:k1, qb(s, half) + 8 * (half - d) - W * i:qb(s, half) + 8 * (half - d) - W * i + 128],
                     came(s, t - 1, a, 32 * i + d, 32 * i + 32, 2), half + k + d == 0, half + k + d == 5]
                    for half in range(2) for k, (i, e, a) in enumerate(four) for d in range(2)], R + ["zq%d.0" % s, "zq%d.1" % s], [pn], ext=ext)
                return offsets(pn, u, 0, 64, nm)
            for k in range(2):
                if k and u == 0 and t: pn = bank("pn")
                pe([[T[pn][:, e * 32:e * 32 + 32], T.zq[k0:k1, z - W * i:z - W * i + 128], came(s, t - 1, a, 32 * i, 32 * i + 32), i == 0, i == 1]
                    for i, e, a in four[2 * k:2 * k + 2]], R + ["zq%d.2" % s], [pn], ext=ext if k or u else None)
                if u == 0 and t: offsets(pn, u, four[2 * k][1] * 32, 32, [nm[four[2 * k][1]]])
            if u or not t: offsets(pn, u, 0, 64, nm)

        def sums(u):
            R, ext, four = sources(u)
            o, pw, apart = col(u) % 128, "pw%d" % (u // 2), u == 3 or u == 0 and t
            names = [["gat%d.%d.%d.%d" % (s, u, half, k) for k in range(32 // UC)] for half in range(2)]
            for half in (rank % 2, 1 - rank % 2) if u == 0 and t else (0, 1):
                for k in range(32 // UC):
                    add("VS", None, ["off%d.%d.%d" % (s, u, half), "tabz%d" % s] + ["tab%d.%d.%d" % (s, i, j) for i in range(2) for j in range(8)],
                        [names[half][k]], UC * 16 * P["c"] * cyc, gat=(s, t, u, half if apart else 0), col=c0 + col(u) + half * 32 + k * UC)
            pe([[T[pw][:, o + e * 32:o + e * 32 + 32], T.zf[k0:k1, W - W * i:W - W * i + 128], came(s, tt, a, 32 * i, 32 * i + 32),
                 tt == t - 1 and k == 0 and u % 2 == 0, False] for tt in ([t - 1] if t else [-1, -2]) for k, (i, e, a) in enumerate(four)],
               R + ["zf0", "zf1"] + ["xl"] * (t == 0), [pw], ext=ext)
            g0 = (c0 + col(u)) * 16
            for half in range(2):
                pe([[T[ph[u]][:, o:o + 64], T.idn[:], T.gat[:, g0 + half * 512 + j:g0 + half * 512 + 512:8] if u == 3 else T.gat[:, g0 + half * 8 + j:g0 + 1024:16],
                     j == 0 and half == 0, j == 7 and half == 1] for j in range(8)], ["idn"] + (names[half] if u == 3 else names[0] + names[1]), [ph[u]])

        def fire(us):
            lo, hi = span(us)
            b, o, n, pw = ph[us[0]], lo % 128, hi - lo, "pw%d" % (us[0] // 2)
            vec({"V": lambda q: q.tensor_scalar(T.rel[:, c0 + lo:c0 + hi], T[b][:, o:o + n], 0.0, 2.0 ** -8, ALU.max, ALU.mult),
                 "S": lambda q: q.activation(T.rel[:, c0 + lo:c0 + hi], T[b][:, o:o + n], ACT.Relu, scale=2.0 ** -8)},
                [], [b, "rel%d.%d" % (s, us[0])], n, eng=P["rel"])
            pe([[T[pw][:, o:o + n], T.polh[:, t0:t0 + 128], T.rel[:, c0 + lo:c0 + hi], False, us[-1] % 2 == 1]], ["polh%d" % s, "rel%d.%d" % (s, us[0])], [pw])

        def changed(us):
            lo, hi = span(us)
            b, o = "pw%d" % (us[0] // 2), lo % 128
            vec({"V": lambda q: q.tensor_scalar(T.vv[:, c0 + lo:c0 + hi], T[b][:, o:o + hi - lo], HALF, None, ALU.add),
                 "S": lambda q: q.activation(T.vv[:, c0 + lo:c0 + hi], T[b][:, o:o + hi - lo], ACT.Identity, bias=HALF)},
                [], [b] + ["vv%d.%d" % (s, u) for u in us], hi - lo, eng=P["vv"])

        def route(cr):
            cc = (rank // 4) ^ cr
            vs, m0, a0, out = T.vv[:, c0 + cc * 128:c0 + cc * 128 + 128], t0 + cc * 64, cc * 64, T.pt[:, 0:64]
            pe([[out, T.ones[0:1, 0:128], T.cst[0:1, :], True, False]], ["ones", "cst"], ["pt"])
            pe([[out, vs, T.zsel[:, k * 64:k * 64 + 64], False, k == 3] for k in range(4)],
               ["zsel0", "zsel1", "vv%d.%d" % (s, 2 * cr), "vv%d.%d" % (s, 2 * cr + 1)], ["pt"], step=4)
            vec(lambda q: q.tensor_tensor(T.mb[:, m0:m0 + 64], out, T.negr[:], ALU.is_equal), ["negr"], ["pt", "mb%d.%d" % (s, cr)], 64)
            if cr == 0: pe([[T.pa[:, 0:128], T.ones[:, 0:128], T.creg[:], True, False]], ["ones", "creg"], ["pa"])
            three = [(0, 0, 64), (32, 0, 32), (0, 32, 32)]
            mms = [[T.pa[:, a0 + o:a0 + o + n], T.tri[:, k * 128:k * 128 + 128], T.mb[:, m0 + i:m0 + i + n], False, False] for k, (o, i, n) in enumerate(three)]
            if cc == 0: mms += [[T.pa[:, 64 + o:64 + o + n], T.ones[:, 0:128], T.mb[:, m0 + i:m0 + i + n], False, False] for o, i, n in three]
            mms[-1][4] = cr == 1
            add("P", lambda q: [q.matmul(*m) for m in mms][-1], ["mb%d.%d" % (s, cr), "tri0", "tri1", "tri2"], ["pa"], 384 * P["pe"] * P["f"])

        vvs = ["vv%d.%d" % (s, u) for u in range(4)]

        def places(k):
            z0 = s * 136
            vec(lambda q: q.tensor_tensor_scan(T.scn[:, z0:z0 + 128], T.dmp[:], T.pa[:, 0:128], -10000.0, ALU.max, ALU.min), ["dmp"], ["pa", "scn%d" % s], 128)
            vec(lambda q: q.tensor_copy(T.ee[:, t0:t0 + 128], T.scn[:, z0:z0 + 136].indirect(T.els[:])), ["scn%d" % s, "els"], ["ee%d" % s], 60 + 128 * P["c"])
            pe([[T.pa[:, 0:16], T.lq[:, 112 - 16 * h:240 - 16 * h], T.ee[:, t0 + h * 16:t0 + (h + 1) * 16], h == 0, h == 7] for h in range(8)],
               ["lq", "ee%d" % s], ["pa"], step=8)
            vec(lambda q: q.tensor_scalar(T.pos[:, s * 16:(s + 1) * 16], T.pa[:, 0:16], 2048.0, None, ALU.add), [], ["pa", "pos%d" % s], 16)
            vec(lambda q: q.tensor_scalar(T.wr[:, c0:c0 + C], T.vv[:, c0:c0 + C], OFFS + 16.0, -16.0, ALU.is_ge, ALU.mult), vvs, ["wr%d" % s], 128)

        for step in steps:
            us = [int(x) for x in step[1:]]
            if step == "|": yield
            elif step == "K": constants()
            else: {"n": numbers, "s": sums, "r": route, "f": fire, "c": changed, "p": policy, "q": places}[step[0]](us if step[0] in "fc" else us[0])
        zero = ["sz%d.%d.%d" % (s, t, r) for r in range(N)]
        for r in range(N):
            gp(lambda q, a=w0 + r * 512: q.iota(T.snd[:, a:a + CAP], [[0, CAP]], 0, 0, **flag), [], [zero[r]], CAP, base=0.13)
        vec(lambda q: q.tensor_tensor(T.snd[:, w0:w0 + SW].indirect(T.pos[:, s * 16:(s + 1) * 16]), T.vv[:, c0:c0 + C], T.wr[:, c0:c0 + C], ALU.add),
            vvs + ["wr%d" % s, "pos%d" % s] + zero, ["snd%d.%d" % (s, t)], 60 + C * P["sc"])
        for x in range(4):
            dsts = [rank ^ rel for rel in (2 * x, 2 * x + 1) if rel]

            def send(q, x=x, dsts=dsts):
                trs = []
                for j, r in enumerate(dsts):
                    rid, pid = topo.addr(T.cores[r])[0:2]
                    eng = topo.engines(core, T.cores[r])
                    eng = eng[j * len(eng) // len(dsts):(j + 1) * len(eng) // len(dsts)]
                    o, lo = w0 + r * 512, (s * RO + t) * S + rank * CAP
                    trs.append(RemoteDMATransfer(dst_ids=[DstId(rid=rid, pnc=pid)], dma_engine_mask=sum(1 << e for e in eng),
                                                 remote_sem=T.sem["ar%d_%d_%d" % (s, t, x)], src=T.snd[:, o:o + CAP], dst=T.lnd[:, lo:lo + CAP]))
                return q.remote_dma_fused(trs, local_sem=T.sem.sent)
            add("G", send, ["snd%d.%d" % (s, t)], [], P["call"], call=len(dsts), st=(s, t, x))

    def last(s):
        for cr in range(2):
            cc = (rank // 4) ^ cr
            pn = bank("pn")
            for u in (2 * cr, 2 * cr + 1):
                i = ((rank // 2) ^ u) % 2
                pe([[T[pn][i * W:(i + 1) * W, e * 64:e * 64 + 64], T.zf[:, W:2 * W], came(s, RO - 1, 4 * cc + 2 * i + e), True, True]
                    for e in range(2)], ["snd%d.%d" % (s, RO - 1)], [pn], ext=(s, RO - 1, u))
            o = s * C + cc * 128
            vec(lambda q, pn=pn, o=o: q.tensor_scalar(T.yo[:, o:o + 128], T[pn][:, 0:128], -float(OFFS), -1.0, ALU.add, ALU.max),
                [], [pn, "yo%d.%d" % (s, cr)], 128)
            for ss, c in [(0, 0), (0, 1), (1, 0)] * (cr == 0) + [(1, 1)] * cr if s else []:
                for i in range(2):
                    a, o = (4 * ((rank // 4) ^ c) + 2 * i) * CAP, ss * C + ((rank // 4) ^ c) * 128
                    dma("YS"[i], T.y[ss * W:(ss + 1) * W, a:a + 128], T.yo[i * W:(i + 1) * W, o:o + 128], ["yo%d.%d" % (ss, c), "yo1.%d" % cr], [], W, 256, sem="st")

    dma("Y", T.plr[:], T.pl[:], [], ["plr"], 128, 256)
    dma("S", T.xs[:], T.x[:], [], ["xs"], 128, 2 * S)
    for s in range(NS):
        tables(s)
        if s == P["polat"]: dma("Y", T.polr[:], T.pol[:], [], ["polr"], 128, 256)
    first_constants()
    copies()
    for s in range(NS): placements(s)
    plies = [ply(s, t) for t in range(RO) for s in range(NS)]
    next(plies[0])
    for k, p in enumerate(plies):
        next(p)
        if k + 1 < len(plies): next(plies[k + 1])
        next(p, None)
    for s in range(NS): last(s)
    return ops


def depend(ops):
    lastw, readers, lastd = {}, {}, {}
    for o in ops:
        d = set()
        for r in o["R"]:
            if r in lastw: d.add(lastw[r])
        for w in o["W"]:
            if w in lastw: d.add(lastw[w])
            d.update(readers.get(w, []))
        for r in o["R"]: readers.setdefault(r, []).append(o["i"])
        for w in o["W"]:
            lastw[w] = o["i"]
            readers[w] = []
        d.discard(o["i"])
        o["deps"] = sorted(d)
        if "sem" in o or "call" in o:
            o["after"] = lastd.get(o["eng"])
            lastd[o["eng"]] = o["i"]


def joins(p, o):
    return "gat" in p and p["gat"] == o["gat"] and abs(p["col"] - o["col"]) == UC


def place(ops, P, order=None, seq=None):
    fin, arr, start, on = {}, {}, {}, {}
    busy = {e: [] for e in "VSPGY"}
    eng, first, pool = 0.0, P["first"], {}
    for o in ops:
        if "gat" in o: pool.setdefault(o["gat"], []).append(o)
    for i, es in order or [(o["i"], o["eng"]) for o in seq or ops]:
        best = None
        for e in es:
            o = pool[ops[i]["gat"]][0 if e == "S" else -1] if "gat" in ops[i] and not order else ops[i]
            d, t = o["dur"], 0.0
            for k in o["deps"]:
                t = max(t, fin[k] + (0.0 if on[k] == e == "P" else P["wake"] if "sem" in ops[k] else P["lat"]))
            if not order and e == "V" and "gat" not in o: t += P["pad"].get(o["W"][-1].split(".")[0], 0.0)
            if o.get("ext"): t = max(t, arr[o["ext"]] + P["wake"])
            if o.get("after") is not None: t = max(t, start[o["after"]] + 1e-3)
            b = busy[e]
            k = len(b)
            while not order and k and b[k - 1][1] > t: k -= 1
            while True:
                if k: t = max(t, b[k - 1][1])
                new = "gat" in o and not (k and t == b[k - 1][1] and joins(ops[b[k - 1][2]], o))
                if k == len(b) or t + d + 0.06 * new <= b[k][0]: break
                k += 1
            x = t + d + 0.06 * new
            cost = x + (P["join"] * new if "gat" in o else P["lean"] * (e == "V"))
            if best is None or cost < best[0]: best = (cost, e, k, t, x, o)
        _, e, k, t, x, o = best
        i = o["i"]
        if "gat" in o: pool[o["gat"]].remove(o)
        busy[e].insert(k, (t, x, i))
        start[i], fin[i], on[i] = t, x, e
        if "sem" in o:
            eng = fin[i] = max(t + P["dma0"], eng) + o["rows"] / 16 * (P["row"] + o["nb"] / P["bw"])
        if "call" in o:
            eng = arr[o["st"]] = max(x + P["dma0"] + first, eng) + 8 * o["call"] * (P["row"] + 128 / P["bw"])
            first = 0.0
    return [(i, on[i]) for i in sorted(start, key=lambda i: (start[i], i))], max(fin.values()), busy


def rank_program(g, core, T, topo):
    rank = T.rank_of(core)
    if rank is None:
        return
    ops = build(T, rank, core, topo, PAR)
    depend(ops)
    queues = {"V": g.vector, "S": g.scalar, "P": g.tensor, "G": g, "Y": g.sync}
    items, item_of, lastq = [], {}, {}
    for i, e in place(ops, PAR)[0]:
        o, p = ops[i], lastq.get(e)
        if "gat" in o and p is not None and joins(p["ops"][-1], o) and all(d in p["deps"] or d in p["seen"] for d in o["deps"]):
            p["ops"].append(o)
        else:
            p = {"ops": [o], "e": e, "k": len(items), "deps": set(o["deps"]), "seen": set(item_of), "inc": False}
            items.append(p)
            lastq[e] = p
        p["deps"].update(o["deps"])
        item_of[i] = p
    known = {e: {} for e in queues}
    for p in items:
        e, kn, waits = p["e"], known[p["e"]], []
        for d in sorted(set(item_of[d]["k"] for d in p["deps"]), reverse=True):
            dp = items[d]
            key = dp["ops"][0].get("sem", dp["e"])
            if key == e == "P" or kn.get(key, -1) >= d: continue
            dp["inc"] = True
            waits.append(dp)
            for k2, v in dp["clock"].items(): kn[k2] = max(kn.get(k2, -1), v)
            kn[key] = max(kn.get(key, -1), d)
        ext = p["ops"][0].get("ext")
        if ext and ext not in kn:
            kn[ext] = 0
            waits.append({"ext": ext})
        p["waits"] = waits
        p["clock"] = dict(kn)
    count = {e: 0 for e in queues}
    sent, stores, engines = 0, 0, len(topo.engines(core, T.cores[rank ^ 1]))
    for p in items:
        e, q, o = p["e"], queues[p["e"]], p["ops"][0]
        for w in p["waits"]:
            if "ext" in w: q.wait_ge(T.sem["ar%d_%d_%d" % w["ext"]], engines)
            elif "sem" in w["ops"][0]: q.wait_ge(T.sem[w["ops"][0]["sem"]], 16)
            else: q.wait_ge(T.sem["e" + w["e"]], w["n"])
        if "gat" in o:
            s = o["gat"][0]
            lo = min(x["col"] for x in p["ops"])
            hi = lo + UC * len(p["ops"])
            win = T.tab[:, s * TB:(s + 1) * TB].indirect(T.off[:, lo:hi])
            out = T.gat[:, lo * 16:hi * 16]
            ins = q.tensor_copy(out, win) if e == "V" else q.activation(out, win, ACT.Copy)
        else:
            ins = (o["fn"][e] if isinstance(o["fn"], dict) else o["fn"])(q)
        if "sem" in o:
            ins.then_inc(T.sem[o["sem"]], 16)
            stores += 16 * (o["sem"] == "st")
        elif "call" in o:
            sent += engines
        elif p["inc"]:
            count[e] += 1
            p["n"] = count[e]
            ins.then_inc(T.sem["e" + e], 1)
    g.wait_ge(T.sem.sent, sent)
    g.sync.wait_ge(T.sem.st, stores)
